import numpy as np
import ml_dtypes


def mxq(x, axis, fmt="e4m3"):
    dtype, down = {"e4m3": (ml_dtypes.float8_e4m3fn, 7), "e5m2": (ml_dtypes.float8_e5m2, 14)}[fmt]
    v = np.moveaxis(np.asarray(x, np.float32).astype(ml_dtypes.bfloat16).astype(np.float64), axis, -1)
    blocks = v.reshape(v.shape[:-1] + (-1, 32))
    amax = np.abs(blocks).max(-1, keepdims=True)
    byte = np.maximum(np.where(amax > 0, np.frexp(amax)[1] - 1 + 127, 0) - down, 1)
    scale = np.exp2(byte - 127.0)
    codes = (blocks / scale).astype(np.float32).astype(dtype).astype(np.float64)
    return np.moveaxis((codes * scale).reshape(v.shape), -1, axis)


WIDE = False


def mx_kscale(k):
    if not WIDE:
        return np.ones(k)
    levels = np.array([10, -10, 5, -5, 0])
    if k % 512:
        return np.exp2(np.random.permutation(np.resize(levels, k // 32))).repeat(32)
    a = np.empty((k // 512, 16))
    for p in range(k // 512):
        a[p, :8] = np.random.permutation(np.resize(levels, 8))
        for g in range(8):
            far = levels[np.abs(levels - a[p, g]) >= 10]
            a[p, g + 8] = far[np.random.randint(len(far))]
    return np.exp2(a.ravel()).repeat(32)


def f64(x):
    return np.asarray(x).astype(np.float64)


def striped(idx):
    return np.tile(idx.reshape(-1, 16).T, (8, 1)).astype(np.uint16)


def unstriped(offs):
    return offs[:16].T.reshape(-1).astype(np.int64)


def striped8(idx):
    return np.concatenate([x.reshape(-1, 16).T for x in idx]).astype(np.uint16)


def runs(offs, k):
    lists = np.stack([offs[16 * r : 16 * r + 16].T.reshape(-1) for r in range(8)]).astype(np.int64)
    return lists[np.arange(k) % 512 // 64]


def pack_weight(w):
    k, n = w.shape
    w = f64(np.asarray(w, np.float32).astype(ml_dtypes.bfloat16)).reshape(k // 32, 32, n)
    amax = np.abs(w).max(1)
    byte = np.clip(np.where(amax > 0, np.frexp(amax)[1] - 1 + 127 - 7, 1), 1, 254)
    scaled = (w * np.exp2(127.0 - byte)[:, None, :]).reshape(k, n).astype(np.float32)
    words = np.ascontiguousarray(scaled.reshape(k // 512, 128, 4, n).transpose(0, 1, 3, 2)).astype(ml_dtypes.float8_e4m3fn).view(np.uint8)
    return words, np.ascontiguousarray(byte.astype(np.uint8).reshape(k // 512, 16, n))


def unpack_weight(words, scales):
    g, p, n, _ = words.shape
    vals = np.ascontiguousarray(words).view(ml_dtypes.float8_e4m3fn).astype(np.float64) * np.repeat(np.exp2(scales.astype(np.float64) - 127.0), 8, axis=1)[..., None]
    return vals.transpose(0, 1, 3, 2).reshape(g * 512, n)

def planes(y):
    n, m = y.shape
    v = y.astype(np.float32).astype(ml_dtypes.bfloat16).astype(np.float64).reshape(n // 32, 32, m)
    top = np.abs(v).max(1)
    byte = np.clip(np.where(top > 0, np.frexp(top)[1] - 1 + 127 - 7, 1), 1, 254)
    codes = (v * np.exp2(127.0 - byte)[:, None, :]).reshape(n, m).astype(np.float32).astype(ml_dtypes.float8_e4m3fn).view(np.uint8)
    words = codes.reshape(n // 512, 128, 4, m).transpose(0, 1, 3, 2)
    return np.ascontiguousarray(words), np.ascontiguousarray(byte.astype(np.uint8).reshape(n // 512, 16, m))


K, T, S, N, U = 512, 2048, 512, 512, 1024


def setup_inputs():
    n = np.random.standard_normal
    s = mx_kscale(K)[:, None]
    packed_xT = pack_weight(n((K, T)) * s)
    return {
        "x_words": packed_xT[0],
        "x_scales": packed_xT[1],
        "w1": (n((K, N)) / np.sqrt(K) / s).astype(np.float32),
        "old": n((N, U)).astype(np.float32),
        "adv": n((N, U)).astype(np.float32),
        "offs": striped(np.random.permutation(T)[:S]),
        "st": striped8(np.stack([np.random.permutation(U)[:S] for _ in range(8)])),
    }


def reference(x_words, x_scales, w1, old, adv, offs, st):
    xq = unpack_weight(x_words, x_scales)[:, unstriped(offs)]
    y = mxq(f64(w1), 0, "e4m3").T @ xq
    rt = np.exp(0.25 * (y - (f64(old)[np.arange(N)[:, None], runs(st, N)])))
    a = f64(adv)[np.arange(N)[:, None], runs(st, N)]
    out_0 = np.minimum(rt * a, np.clip(rt, 0.8, 1.25) * a)
    return (out_0,) + planes(out_0)

@@ -1,0 +1,149 @@
+from contextlib import ExitStack
+
+import concourse.mybir as mybir
+
+K, T, S, N, U = 512, 2048, 512, 512, 1024
+FLOPS = 2 * K * N * S
+
+F32 = mybir.dt.float32
+BF16 = mybir.dt.bfloat16
+I32 = mybir.dt.int32
+U32 = mybir.dt.uint32
+U16 = mybir.dt.uint16
+U8 = mybir.dt.uint8
+FP8X4 = mybir.dt.float8_e4m3fn_x4
+ALU = mybir.AluOpType
+ACT = mybir.ActivationFunctionType
+
+P = 128
+PACK = 4
+HALF = S // 2
+CLIP_LO, CLIP_HI = 0.8, 1.25
+
+
+def tile_picked_ppo8_none_po_kernel(tc, x_words, x_scales, w1, old, adv, offs, st, out_0, out_1, out_2):
+    nc = tc.nc
+    with ExitStack() as ctx:
+        sb = ctx.enter_context(tc.tile_pool(name="sb", bufs=1))
+        psum = ctx.enter_context(tc.psum_pool(name="psum", bufs=1))
+
+        def tiles(name, count, shape, dtype):
+            return [sb.tile(shape, dtype, name="%s%d" % (name, i), align_bytes=64) for i in range(count)]
+
+        halves = [slice(h * HALF, (h + 1) * HALF) for h in range(2)]
+        list_halves = [slice(h * HALF // 16, (h + 1) * HALF // 16) for h in range(2)]
+
+        offs_sb = sb.tile([P, S // 16], U16, name="offs_sb")
+        st_sb = sb.tile([P, S // 16], U16, name="st_sb")
+        xw = sb.tile([P, T], U32, name="xw", align_bytes=64)
+        xs = sb.tile([P, T], U8, name="xs", align_bytes=64)
+        w_raw = tiles("w_raw", 2, [P, PACK, N // 2], F32)
+        adv_sb = tiles("adv_sb", PACK, [P, U], F32)
+        old_sb = tiles("old_sb", PACK, [P, U], F32)
+
+        adv_rows = adv.rearrange("(p t) u -> p t u", t=PACK)
+        old_rows = old.rearrange("(p t) u -> p t u", t=PACK)
+        w_rows = w1.rearrange("(p j) c -> p j c", j=PACK)
+        out_rows = out_0.rearrange("(p t) j -> p t j", t=PACK)
+
+        nc.vector.memset(xs[:].bitcast(I32), 0)
+        nc.sync.dma_start(st_sb[:], st)
+        nc.sync.dma_start(offs_sb[:], offs)
+        nc.sync.dma_start(adv_sb[0][:], adv_rows[:, 0, :])
+        for q in range(4):
+            nc.sync.dma_start(xs[32 * q : 32 * q + 4, :].bitcast(I32), x_scales[0].bitcast(I32)[4 * q : 4 * q + 4, :])
+        nc.sync.dma_start(adv_sb[1][:], adv_rows[:, 1, :])
+        nc.sync.dma_start(w_raw[0][:], w_rows[:, :, 0 : N // 2])
+        nc.sync.dma_start(adv_sb[2][:], adv_rows[:, 2, :])
+        nc.sync.dma_start(w_raw[1][:], w_rows[:, :, N // 2 : N])
+        nc.sync.dma_start(xw[:].bitcast(I32), x_words[0].rearrange("p c r -> p (c r)").bitcast(I32))
+        nc.sync.dma_start(adv_sb[3][:], adv_rows[:, 3, :])
+        for t in range(PACK):
+            nc.sync.dma_start(old_sb[t][:], old_rows[:, t, :])
+
+        a = tiles("a", PACK, [P, S], F32)
+        cap = tiles("cap", PACK, [P, S], F32)
+
+        def fetch_adv(t):
+            for h in range(2):
+                nc.vector.tensor_copy(a[t][:, halves[h]], adv_sb[t][:].indirect(st_sb[:, list_halves[h]]))
+            for h in range(2):
+                nc.vector.scalar_tensor_tensor(
+                    cap[t][:, halves[h]], a[t][:, halves[h]], CLIP_LO / CLIP_HI, a[t][:, halves[h]], ALU.mult, ALU.max
+                )
+
+        xg_scales = sb.tile([P, S], U8, name="xg_scales", align_bytes=64)
+        xg_words = sb.tile([P, S], U32, name="xg_words", align_bytes=64)
+        nc.vector.tensor_copy(xg_scales[:], xs[:].indirect(offs_sb[:]))
+        for t in range(PACK - 1):
+            fetch_adv(t)
+
+        w_bf = sb.tile([P, PACK * N], BF16, name="w_bf", align_bytes=64)
+        w_dealt = w_bf[:].rearrange("p (t m j) -> p m j t", t=PACK, j=PACK)
+        for h in range(2):
+            nc.scalar.copy(w_dealt[:, h * P // 2 : (h + 1) * P // 2, :, :], w_raw[h][:].rearrange("p j (m t) -> p m j t", t=PACK))
+        w_codes = sb.tile([P, N], U32, name="w_codes", align_bytes=64)
+        w_scales = sb.tile([P, N], U8, name="w_scales", align_bytes=64)
+        nc.vector.quantize_mx(out=w_codes[:].bitcast(FP8X4), scales=w_scales[:], in_=w_bf[:])
+        nc.vector.tensor_copy(xg_words[:], xw[:].indirect(offs_sb[:]))
+        fetch_adv(PACK - 1)
+
+        y = tiles("y", PACK + 1, [P, S], F32)
+        for t in range(PACK):
+            bank = psum.tile([P, S], F32, name="bank%d" % t)
+            cols = slice(t * P, (t + 1) * P)
+            nc.tensor.matmul_mx(
+                out=bank[:],
+                lhsT=w_codes[:, cols].bitcast(FP8X4),
+                lhsT_scale=w_scales[:, cols],
+                rhs=xg_words[:].bitcast(FP8X4),
+                rhs_scale=xg_scales[:],
+                start=True,
+                stop=True,
+            )
+            nc.scalar.copy(y[t][:], bank[:])
+
+        diff = tiles("diff", PACK, [P, S], F32)
+        ratio = tiles("ratio", PACK, [P, S], F32)
+        res = tiles("res", 2, [P, PACK, HALF], F32)
+
+        def fetch_old(t):
+            nc.vector.tensor_tensor(diff[t][:], old_sb[t][:].indirect(st_sb[:]), y[t][:], ALU.subtract)
+            nc.scalar.activation(ratio[t][:], diff[t][:], ACT.Exp, scale=-0.25)
+
+        def finish(t):
+            plain = y[t + 1]
+            for h in range(2):
+                nc.vector.tensor_tensor(plain[:, halves[h]], ratio[t][:, halves[h]], a[t][:, halves[h]], ALU.mult)
+            for h in range(2):
+                nc.vector.scalar_tensor_tensor(
+                    res[h][:, t, :], cap[t][:, halves[h]], CLIP_HI, plain[:, halves[h]], ALU.mult, ALU.min
+                )
+            for h in range(2):
+                nc.sync.dma_start(out_rows[:, t, halves[h]], res[h][:, t, :])
+
+        fetch_old(0)
+        for t in range(1, PACK):
+            fetch_old(t)
+            finish(t - 1)
+        finish(PACK - 1)
+
+        res_bf = tiles("res_bf", 2, [P, HALF, PACK], BF16)
+        codes = tiles("codes", 2, [P, HALF], U32)
+        scales = sb.tile([P, S], U8, name="scales", align_bytes=64)
+        words_out = out_1[0].rearrange("p c r -> p (c r)").bitcast(I32)
+        for h, copy in enumerate((nc.scalar.copy, nc.vector.tensor_copy)):
+            copy(
+                res_bf[h][:].rearrange("p (c i) t -> p c t i", i=4),
+                res[h][:].rearrange("p t (c i) -> p c t i", i=4),
+            )
+        for h in range(2):
+            nc.vector.quantize_mx(
+                out=codes[h][:].bitcast(FP8X4),
+                scales=scales[:, halves[h]],
+                in_=res_bf[h][:].rearrange("p c t -> p (c t)"),
+            )
+            nc.sync.dma_start(words_out[:, halves[h]], codes[h][:].bitcast(I32))
+        for q in range(4):
+            queue = nc.scalar if q % 2 else nc.sync
+            queue.dma_start(out_2[0].bitcast(I32)[4 * q : 4 * q + 4, :], scales[32 * q : 32 * q + 4, :].bitcast(I32))

@@ -1,6 +1,7 @@
 from contextlib import ExitStack
 
 import concourse.mybir as mybir
+from concourse.masks import make_identity
 
 K, T, S, N, U = 512, 2048, 512, 512, 1024
 FLOPS = 2 * K * N * S
@@ -19,6 +20,8 @@ P = 128
 PACK = 4
 HALF = S // 2
 CLIP_LO, CLIP_HI = 0.8, 1.25
+W_SPLIT = 64
+CAST_SPLIT = 192
 
 
 def tile_picked_ppo8_none_po_kernel(tc, x_words, x_scales, w1, old, adv, offs, st, out_0, out_1, out_2):
@@ -37,7 +40,7 @@ def tile_picked_ppo8_none_po_kernel(tc, x_words, x_scales, w1, old, adv, offs, s
         st_sb = sb.tile([P, S // 16], U16, name="st_sb")
         xw = sb.tile([P, T], U32, name="xw", align_bytes=64)
         xs = sb.tile([P, T], U8, name="xs", align_bytes=64)
-        w_raw = tiles("w_raw", 2, [P, PACK, N // 2], F32)
+        w_raw = sb.tile([P, PACK, N], F32, name="w_raw", align_bytes=64)
         adv_sb = tiles("adv_sb", PACK, [P, U], F32)
         old_sb = tiles("old_sb", PACK, [P, U], F32)
 
@@ -46,97 +49,138 @@ def tile_picked_ppo8_none_po_kernel(tc, x_words, x_scales, w1, old, adv, offs, s
         w_rows = w1.rearrange("(p j) c -> p j c", j=PACK)
         out_rows = out_0.rearrange("(p t) j -> p t j", t=PACK)
 
-        nc.vector.memset(xs[:].bitcast(I32), 0)
+        nc.gpsimd.memset(xs[:].bitcast(I32)[:, 0 : T // 8], 0)
+        nc.vector.memset(xs[:].bitcast(I32)[:, T // 8 : T // 4], 0)
+        ident = sb.tile([P, P], F32, name="ident", align_bytes=64)
+        make_identity(nc, ident[:])
+        nc.sync.dma_start(adv_sb[0][:], adv_rows[:, 0, :])
         nc.sync.dma_start(st_sb[:], st)
         nc.sync.dma_start(offs_sb[:], offs)
-        nc.sync.dma_start(adv_sb[0][:], adv_rows[:, 0, :])
-        for q in range(4):
-            nc.sync.dma_start(xs[32 * q : 32 * q + 4, :].bitcast(I32), x_scales[0].bitcast(I32)[4 * q : 4 * q + 4, :])
+        for r in range(4):
+            nc.sync.dma_start(xs[r:P:32, :].bitcast(I32), x_scales[0].bitcast(I32)[r:16:4, :])
+        nc.sync.dma_start(w_raw[:], w_rows)
         nc.sync.dma_start(adv_sb[1][:], adv_rows[:, 1, :])
-        nc.sync.dma_start(w_raw[0][:], w_rows[:, :, 0 : N // 2])
-        nc.sync.dma_start(adv_sb[2][:], adv_rows[:, 2, :])
-        nc.sync.dma_start(w_raw[1][:], w_rows[:, :, N // 2 : N])
         nc.sync.dma_start(xw[:].bitcast(I32), x_words[0].rearrange("p c r -> p (c r)").bitcast(I32))
+        nc.sync.dma_start(adv_sb[2][:], adv_rows[:, 2, :])
+        nc.sync.dma_start(old_sb[0][:], old_rows[:, 0, :])
         nc.sync.dma_start(adv_sb[3][:], adv_rows[:, 3, :])
-        for t in range(PACK):
+        for t in range(1, PACK):
             nc.sync.dma_start(old_sb[t][:], old_rows[:, t, :])
 
-        a = tiles("a", PACK, [P, S], F32)
-        cap = tiles("cap", PACK, [P, S], F32)
+        y = tiles("y", PACK, [P, S], F32)
+        a = tiles("a", PACK - 1, [P, S], F32) + y[0:1]
+        low_t = [w_raw[:, 0, :], w_raw[:, 2, :]] + [x[:] for x in tiles("low_t", 2, [P, S], F32)]
+        rise_t = [w_raw[:, 1, :], w_raw[:, 3, :]] + [x[:] for x in tiles("rise_t", 2, [P, S], F32)]
+        cap = [psum.tile([P, S], F32, name="cap%d" % t) for t in range(PACK)]
+        blocks = [slice(c * P, (c + 1) * P) for c in range(S // P)]
 
         def fetch_adv(t):
-            for h in range(2):
-                nc.vector.tensor_copy(a[t][:, halves[h]], adv_sb[t][:].indirect(st_sb[:, list_halves[h]]))
-            for h in range(2):
-                nc.vector.scalar_tensor_tensor(
-                    cap[t][:, halves[h]], a[t][:, halves[h]], CLIP_LO / CLIP_HI, a[t][:, halves[h]], ALU.mult, ALU.max
-                )
+            if t < PACK - 1:
+                nc.vector.tensor_copy(a[t][:], adv_sb[t][:].indirect(st_sb[:]))
+            else:
+                for h in range(2):
+                    nc.vector.tensor_copy(a[t][:, halves[h]], adv_sb[t][:].indirect(st_sb[:, list_halves[h]]))
+            a_t = psum.tile([P, S], F32, name="a_t", bufs=3)
+            for b in blocks:
+                nc.tensor.transpose(a_t[:, b], a[t][:, b], ident[:])
+            nc.scalar.activation(low_t[t], a_t[:], ACT.Copy, scale=CLIP_LO)
+            nc.scalar.activation(rise_t[t], a_t[:], ACT.Relu, scale=CLIP_HI - CLIP_LO)
+            for b in blocks:
+                nc.tensor.matmul(cap[t][:, b], low_t[t][:, b], ident[:], start=True, stop=False, is_transpose=True)
+                nc.tensor.matmul(cap[t][:, b], rise_t[t][:, b], ident[:], start=False, stop=True, is_transpose=True)
 
         xg_scales = sb.tile([P, S], U8, name="xg_scales", align_bytes=64)
         xg_words = sb.tile([P, S], U32, name="xg_words", align_bytes=64)
         nc.vector.tensor_copy(xg_scales[:], xs[:].indirect(offs_sb[:]))
-        for t in range(PACK - 1):
-            fetch_adv(t)
 
         w_bf = sb.tile([P, PACK * N], BF16, name="w_bf", align_bytes=64)
-        w_dealt = w_bf[:].rearrange("p (t m j) -> p m j t", t=PACK, j=PACK)
-        for h in range(2):
-            nc.scalar.copy(w_dealt[:, h * P // 2 : (h + 1) * P // 2, :, :], w_raw[h][:].rearrange("p j (m t) -> p m j t", t=PACK))
+        w_dealt = w_bf[:].rearrange("p (t m j) -> p t m j", t=PACK, j=PACK)
+        w_plain = w_raw[:].rearrange("p j (m t) -> p t m j", t=PACK)
+        nc.vector.tensor_copy(w_dealt[:, :, 0:W_SPLIT, :], w_plain[:, :, 0:W_SPLIT, :])
+        nc.scalar.copy(w_dealt[:, :, W_SPLIT:P, :], w_plain[:, :, W_SPLIT:P, :])
         w_codes = sb.tile([P, N], U32, name="w_codes", align_bytes=64)
         w_scales = sb.tile([P, N], U8, name="w_scales", align_bytes=64)
         nc.vector.quantize_mx(out=w_codes[:].bitcast(FP8X4), scales=w_scales[:], in_=w_bf[:])
-        nc.vector.tensor_copy(xg_words[:], xw[:].indirect(offs_sb[:]))
-        fetch_adv(PACK - 1)
+        for h in range(2):
+            nc.vector.tensor_copy(xg_words[:, halves[h]], xw[:].indirect(offs_sb[:, list_halves[h]]))
 
-        y = tiles("y", PACK + 1, [P, S], F32)
-        for t in range(PACK):
-            bank = psum.tile([P, S], F32, name="bank%d" % t)
+        plain = y[1:] + tiles("plain", 1, [P, S], F32)
+        first_bank = psum.tile([P, S], F32, name="first_bank")
+
+        def project(t, bank, picked):
             cols = slice(t * P, (t + 1) * P)
             nc.tensor.matmul_mx(
-                out=bank[:],
+                out=bank[:, picked],
                 lhsT=w_codes[:, cols].bitcast(FP8X4),
                 lhsT_scale=w_scales[:, cols],
-                rhs=xg_words[:].bitcast(FP8X4),
-                rhs_scale=xg_scales[:],
+                rhs=xg_words[:, picked].bitcast(FP8X4),
+                rhs_scale=xg_scales[:, picked],
                 start=True,
                 stop=True,
             )
-            nc.scalar.copy(y[t][:], bank[:])
+            nc.scalar.copy(y[t][:, picked], bank[:, picked])
+
+        project(0, first_bank, halves[0])
+        project(0, cap[0], halves[1])
+        for t in range(1, PACK):
+            project(t, cap[t], slice(0, S))
 
         diff = tiles("diff", PACK, [P, S], F32)
         ratio = tiles("ratio", PACK, [P, S], F32)
         res = tiles("res", 2, [P, PACK, HALF], F32)
 
         def fetch_old(t):
-            nc.vector.tensor_tensor(diff[t][:], old_sb[t][:].indirect(st_sb[:]), y[t][:], ALU.subtract)
-            nc.scalar.activation(ratio[t][:], diff[t][:], ACT.Exp, scale=-0.25)
-
-        def finish(t):
-            plain = y[t + 1]
             for h in range(2):
-                nc.vector.tensor_tensor(plain[:, halves[h]], ratio[t][:, halves[h]], a[t][:, halves[h]], ALU.mult)
-            for h in range(2):
-                nc.vector.scalar_tensor_tensor(
-                    res[h][:, t, :], cap[t][:, halves[h]], CLIP_HI, plain[:, halves[h]], ALU.mult, ALU.min
+                nc.vector.tensor_tensor(
+                    diff[t][:, halves[h]], old_sb[t][:].indirect(st_sb[:, list_halves[h]]), y[t][:, halves[h]], ALU.subtract
                 )
             for h in range(2):
-                nc.sync.dma_start(out_rows[:, t, halves[h]], res[h][:, t, :])
+                nc.scalar.activation(ratio[t][:, halves[h]], diff[t][:, halves[h]], ACT.Exp, scale=-0.25)
+
+        def product(t, h):
+            nc.vector.tensor_tensor(plain[t][:, halves[h]], ratio[t][:, halves[h]], a[t][:, halves[h]], ALU.mult)
+
+        def smaller(t, h):
+            nc.vector.tensor_tensor(res[h][:, t, :], cap[t][:, halves[h]], plain[t][:, halves[h]], ALU.min)
+            nc.sync.dma_start(out_rows[:, t, halves[h]], res[h][:, t, :])
+
+        for t in range(PACK - 1):
+            fetch_adv(t)
+        def finish(t):
+            for step in (product, smaller):
+                for h in range(2):
+                    step(t, h)
 
         fetch_old(0)
-        for t in range(1, PACK):
-            fetch_old(t)
-            finish(t - 1)
-        finish(PACK - 1)
+        fetch_adv(PACK - 1)
+        fetch_old(1)
+        finish(0)
+        fetch_old(2)
+        finish(1)
+        fetch_old(3)
+        product(2, 0)
+        product(2, 1)
+        smaller(2, 0)
+        product(3, 0)
+        product(3, 1)
+        smaller(3, 0)
+        smaller(2, 1)
+        smaller(3, 1)
 
         res_bf = tiles("res_bf", 2, [P, HALF, PACK], BF16)
         codes = tiles("codes", 2, [P, HALF], U32)
         scales = sb.tile([P, S], U8, name="scales", align_bytes=64)
         words_out = out_1[0].rearrange("p c r -> p (c r)").bitcast(I32)
-        for h, copy in enumerate((nc.scalar.copy, nc.vector.tensor_copy)):
+
+        def round_and_weave(copy, h, cols):
             copy(
-                res_bf[h][:].rearrange("p (c i) t -> p c t i", i=4),
-                res[h][:].rearrange("p t (c i) -> p c t i", i=4),
+                res_bf[h][:, cols, :].rearrange("p (c i) t -> p c t i", i=4),
+                res[h][:, :, cols].rearrange("p t (c i) -> p c t i", i=4),
             )
+
+        round_and_weave(nc.scalar.copy, 0, slice(0, CAST_SPLIT))
+        round_and_weave(nc.vector.tensor_copy, 0, slice(CAST_SPLIT, HALF))
+        round_and_weave(nc.vector.tensor_copy, 1, slice(0, HALF))
         for h in range(2):
             nc.vector.quantize_mx(
                 out=codes[h][:].bitcast(FP8X4),
@@ -144,6 +188,6 @@ def tile_picked_ppo8_none_po_kernel(tc, x_words, x_scales, w1, old, adv, offs, s
                 in_=res_bf[h][:].rearrange("p c t -> p (c t)"),
             )
             nc.sync.dma_start(words_out[:, halves[h]], codes[h][:].bitcast(I32))
-        for q in range(4):
-            queue = nc.scalar if q % 2 else nc.sync
-            queue.dma_start(out_2[0].bitcast(I32)[4 * q : 4 * q + 4, :], scales[32 * q : 32 * q + 4, :].bitcast(I32))
+        for r in range(4):
+            queue = nc.scalar if r % 2 else nc.sync
+            queue.dma_start(out_2[0].bitcast(I32)[r:16:4, :], scales[r:P:32, :].bitcast(I32))

@@ -18,10 +18,13 @@ ACT = mybir.ActivationFunctionType
 
 P = 128
 PACK = 4
+QUADRANT = 32
+GROUP = 16
 HALF = S // 2
+LINE = 4
+A_T_BANKS = 3
 CLIP_LO, CLIP_HI = 0.8, 1.25
-W_SPLIT = 64
-CAST_SPLIT = 192
+RATIO_SCALE = 0.25
 
 
 def tile_picked_ppo8_none_po_kernel(tc, x_words, x_scales, w1, old, adv, offs, st, out_0, out_1, out_2):
@@ -34,10 +37,10 @@ def tile_picked_ppo8_none_po_kernel(tc, x_words, x_scales, w1, old, adv, offs, s
             return [sb.tile(shape, dtype, name="%s%d" % (name, i), align_bytes=64) for i in range(count)]
 
         halves = [slice(h * HALF, (h + 1) * HALF) for h in range(2)]
-        list_halves = [slice(h * HALF // 16, (h + 1) * HALF // 16) for h in range(2)]
+        list_halves = [slice(h * HALF // GROUP, (h + 1) * HALF // GROUP) for h in range(2)]
 
-        offs_sb = sb.tile([P, S // 16], U16, name="offs_sb")
-        st_sb = sb.tile([P, S // 16], U16, name="st_sb")
+        offs_sb = sb.tile([P, S // GROUP], U16, name="offs_sb")
+        st_sb = sb.tile([P, S // GROUP], U16, name="st_sb")
         xw = sb.tile([P, T], U32, name="xw", align_bytes=64)
         xs = sb.tile([P, T], U8, name="xs", align_bytes=64)
         w_raw = sb.tile([P, PACK, N], F32, name="w_raw", align_bytes=64)
@@ -49,38 +52,35 @@ def tile_picked_ppo8_none_po_kernel(tc, x_words, x_scales, w1, old, adv, offs, s
         w_rows = w1.rearrange("(p j) c -> p j c", j=PACK)
         out_rows = out_0.rearrange("(p t) j -> p t j", t=PACK)
 
-        nc.gpsimd.memset(xs[:].bitcast(I32)[:, 0 : T // 8], 0)
-        nc.vector.memset(xs[:].bitcast(I32)[:, T // 8 : T // 4], 0)
+        xs_words = xs[:].bitcast(I32)
+        nc.gpsimd.memset(xs_words[:, 0 : T // 8], 0)
+        nc.vector.memset(xs_words[:, T // 8 : T // 4], 0)
         ident = sb.tile([P, P], F32, name="ident", align_bytes=64)
         make_identity(nc, ident[:])
+
         nc.sync.dma_start(adv_sb[0][:], adv_rows[:, 0, :])
         nc.sync.dma_start(st_sb[:], st)
         nc.sync.dma_start(offs_sb[:], offs)
-        for r in range(4):
-            nc.sync.dma_start(xs[r:P:32, :].bitcast(I32), x_scales[0].bitcast(I32)[r:16:4, :])
+        for r in range(PACK):
+            nc.sync.dma_start(xs[r:P:QUADRANT, :].bitcast(I32), x_scales[0].bitcast(I32)[r : K // 32 : PACK, :])
         nc.sync.dma_start(w_raw[:], w_rows)
         nc.sync.dma_start(adv_sb[1][:], adv_rows[:, 1, :])
         nc.sync.dma_start(xw[:].bitcast(I32), x_words[0].rearrange("p c r -> p (c r)").bitcast(I32))
         nc.sync.dma_start(adv_sb[2][:], adv_rows[:, 2, :])
-        nc.sync.dma_start(old_sb[0][:], old_rows[:, 0, :])
         nc.sync.dma_start(adv_sb[3][:], adv_rows[:, 3, :])
-        for t in range(1, PACK):
+        for t in range(PACK):
             nc.sync.dma_start(old_sb[t][:], old_rows[:, t, :])
 
         y = tiles("y", PACK, [P, S], F32)
-        a = tiles("a", PACK - 1, [P, S], F32) + y[0:1]
+        a = tiles("a", PACK, [P, S], F32)
         low_t = [w_raw[:, 0, :], w_raw[:, 2, :]] + [x[:] for x in tiles("low_t", 2, [P, S], F32)]
         rise_t = [w_raw[:, 1, :], w_raw[:, 3, :]] + [x[:] for x in tiles("rise_t", 2, [P, S], F32)]
         cap = [psum.tile([P, S], F32, name="cap%d" % t) for t in range(PACK)]
         blocks = [slice(c * P, (c + 1) * P) for c in range(S // P)]
 
         def fetch_adv(t):
-            if t < PACK - 1:
-                nc.vector.tensor_copy(a[t][:], adv_sb[t][:].indirect(st_sb[:]))
-            else:
-                for h in range(2):
-                    nc.vector.tensor_copy(a[t][:, halves[h]], adv_sb[t][:].indirect(st_sb[:, list_halves[h]]))
-            a_t = psum.tile([P, S], F32, name="a_t", bufs=3)
+            nc.vector.tensor_copy(a[t][:], adv_sb[t][:].indirect(st_sb[:]))
+            a_t = psum.tile([P, S], F32, name="a_t", bufs=A_T_BANKS)
             for b in blocks:
                 nc.tensor.transpose(a_t[:, b], a[t][:, b], ident[:])
             nc.scalar.activation(low_t[t], a_t[:], ACT.Copy, scale=CLIP_LO)
@@ -96,8 +96,8 @@ def tile_picked_ppo8_none_po_kernel(tc, x_words, x_scales, w1, old, adv, offs, s
         w_bf = sb.tile([P, PACK * N], BF16, name="w_bf", align_bytes=64)
         w_dealt = w_bf[:].rearrange("p (t m j) -> p t m j", t=PACK, j=PACK)
         w_plain = w_raw[:].rearrange("p j (m t) -> p t m j", t=PACK)
-        nc.vector.tensor_copy(w_dealt[:, :, 0:W_SPLIT, :], w_plain[:, :, 0:W_SPLIT, :])
-        nc.scalar.copy(w_dealt[:, :, W_SPLIT:P, :], w_plain[:, :, W_SPLIT:P, :])
+        nc.vector.tensor_copy(w_dealt[:, :, 0 : P // 2, :], w_plain[:, :, 0 : P // 2, :])
+        nc.scalar.copy(w_dealt[:, :, P // 2 : P, :], w_plain[:, :, P // 2 : P, :])
         w_codes = sb.tile([P, N], U32, name="w_codes", align_bytes=64)
         w_scales = sb.tile([P, N], U8, name="w_scales", align_bytes=64)
         nc.vector.quantize_mx(out=w_codes[:].bitcast(FP8X4), scales=w_scales[:], in_=w_bf[:])
@@ -135,52 +135,57 @@ def tile_picked_ppo8_none_po_kernel(tc, x_words, x_scales, w1, old, adv, offs, s
                     diff[t][:, halves[h]], old_sb[t][:].indirect(st_sb[:, list_halves[h]]), y[t][:, halves[h]], ALU.subtract
                 )
             for h in range(2):
-                nc.scalar.activation(ratio[t][:, halves[h]], diff[t][:, halves[h]], ACT.Exp, scale=-0.25)
+                nc.scalar.activation(ratio[t][:, halves[h]], diff[t][:, halves[h]], ACT.Exp, scale=-RATIO_SCALE)
 
         def product(t, h):
             nc.vector.tensor_tensor(plain[t][:, halves[h]], ratio[t][:, halves[h]], a[t][:, halves[h]], ALU.mult)
 
-        def smaller(t, h):
-            nc.vector.tensor_tensor(res[h][:, t, :], cap[t][:, halves[h]], plain[t][:, halves[h]], ALU.min)
-            nc.sync.dma_start(out_rows[:, t, halves[h]], res[h][:, t, :])
+        def smaller(t, h, part):
+            cols = slice(h * HALF + part.start, h * HALF + part.stop)
+            nc.vector.tensor_tensor(res[h][:, t, part], cap[t][:, cols], plain[t][:, cols], ALU.min)
 
-        for t in range(PACK - 1):
+        def store_pair(t, h):
+            nc.sync.dma_start(out_rows[:, t : t + 2, halves[h]], res[h][:, t : t + 2, :])
+
+        whole = slice(0, HALF)
+        parts = [slice(0, HALF // 2), slice(HALF // 2, HALF)]
+
+        for t in range(PACK):
             fetch_adv(t)
-        def finish(t):
-            for step in (product, smaller):
-                for h in range(2):
-                    step(t, h)
 
         fetch_old(0)
-        fetch_adv(PACK - 1)
-        fetch_old(1)
-        finish(0)
-        fetch_old(2)
-        finish(1)
+        for t in range(2):
+            fetch_old(t + 1)
+            for h in range(2):
+                product(t, h)
+            for h in range(2):
+                smaller(t, h, whole)
+        for h in range(2):
+            store_pair(0, h)
         fetch_old(3)
-        product(2, 0)
-        product(2, 1)
-        smaller(2, 0)
-        product(3, 0)
-        product(3, 1)
-        smaller(3, 0)
-        smaller(2, 1)
-        smaller(3, 1)
+
+        for h, pieces in ((0, [whole]), (1, parts)):
+            for t in (2, 3):
+                product(t, h)
+            for part in pieces:
+                for t in (2, 3):
+                    smaller(t, h, part)
+            store_pair(2, h)
 
         res_bf = tiles("res_bf", 2, [P, HALF, PACK], BF16)
         codes = tiles("codes", 2, [P, HALF], U32)
         scales = sb.tile([P, S], U8, name="scales", align_bytes=64)
         words_out = out_1[0].rearrange("p c r -> p (c r)").bitcast(I32)
 
-        def round_and_weave(copy, h, cols):
+        def round_and_weave(copy, h, part):
             copy(
-                res_bf[h][:, cols, :].rearrange("p (c i) t -> p c t i", i=4),
-                res[h][:, :, cols].rearrange("p t (c i) -> p c t i", i=4),
+                res_bf[h][:, part, :].rearrange("p (c i) t -> p c t i", i=LINE),
+                res[h][:, :, part].rearrange("p t (c i) -> p c t i", i=LINE),
             )
 
-        round_and_weave(nc.scalar.copy, 0, slice(0, CAST_SPLIT))
-        round_and_weave(nc.vector.tensor_copy, 0, slice(CAST_SPLIT, HALF))
-        round_and_weave(nc.vector.tensor_copy, 1, slice(0, HALF))
+        round_and_weave(nc.scalar.copy, 0, whole)
+        for part in parts:
+            round_and_weave(nc.vector.tensor_copy, 1, part)
         for h in range(2):
             nc.vector.quantize_mx(
                 out=codes[h][:].bitcast(FP8X4),
@@ -188,6 +193,6 @@ def tile_picked_ppo8_none_po_kernel(tc, x_words, x_scales, w1, old, adv, offs, s
                 in_=res_bf[h][:].rearrange("p c t -> p (c t)"),
             )
             nc.sync.dma_start(words_out[:, halves[h]], codes[h][:].bitcast(I32))
-        for r in range(4):
+        for r in range(PACK):
             queue = nc.scalar if r % 2 else nc.sync
-            queue.dma_start(out_2[0].bitcast(I32)[r:16:4, :], scales[r:P:32, :].bitcast(I32))
+            queue.dma_start(out_2[0].bitcast(I32)[r : N // 32 : PACK, :], scales[r:P:QUADRANT, :].bitcast(I32))

@@ -104,7 +104,6 @@ def tile_picked_ppo8_none_po_kernel(tc, x_words, x_scales, w1, old, adv, offs, s
         for h in range(2):
             nc.vector.tensor_copy(xg_words[:, halves[h]], xw[:].indirect(offs_sb[:, list_halves[h]]))
 
-        plain = y[1:] + tiles("plain", 1, [P, S], F32)
         first_bank = psum.tile([P, S], F32, name="first_bank")
 
         def project(t, bank, picked):
@@ -127,50 +126,54 @@ def tile_picked_ppo8_none_po_kernel(tc, x_words, x_scales, w1, old, adv, offs, s
 
         diff = tiles("diff", PACK, [P, S], F32)
         ratio = tiles("ratio", PACK, [P, S], F32)
-        res = tiles("res", 2, [P, PACK, HALF], F32)
+        plain = tiles("plain", PACK, [P, S], F32)
+        res = sb.tile([P, 2, PACK, HALF], F32, name="res", align_bytes=64)
 
-        def fetch_old(t):
-            for h in range(2):
-                nc.vector.tensor_tensor(
-                    diff[t][:, halves[h]], old_sb[t][:].indirect(st_sb[:, list_halves[h]]), y[t][:, halves[h]], ALU.subtract
-                )
-            for h in range(2):
-                nc.scalar.activation(ratio[t][:, halves[h]], diff[t][:, halves[h]], ACT.Exp, scale=-RATIO_SCALE)
+        def fetch_old(t, pieces):
+            for cols in pieces:
+                entries = slice(cols.start // GROUP, cols.stop // GROUP)
+                nc.vector.tensor_tensor(diff[t][:, cols], old_sb[t][:].indirect(st_sb[:, entries]), y[t][:, cols], ALU.subtract)
+            for cols in pieces:
+                nc.scalar.activation(ratio[t][:, cols], diff[t][:, cols], ACT.Exp, scale=-RATIO_SCALE)
 
-        def product(t, h):
-            nc.vector.tensor_tensor(plain[t][:, halves[h]], ratio[t][:, halves[h]], a[t][:, halves[h]], ALU.mult)
+        def product(t, cols):
+            nc.vector.tensor_tensor(plain[t][:, cols], ratio[t][:, cols], a[t][:, cols], ALU.mult)
+
+        def by_halves(tile):
+            return tile[:].rearrange("p (h c) -> p h c", h=2)
 
         def smaller(t, h, part):
-            cols = slice(h * HALF + part.start, h * HALF + part.stop)
-            nc.vector.tensor_tensor(res[h][:, t, part], cap[t][:, cols], plain[t][:, cols], ALU.min)
+            nc.vector.tensor_tensor(res[:, h, t, part], by_halves(cap[t])[:, h, part], by_halves(plain[t])[:, h, part], ALU.min)
 
-        def store_pair(t, h):
-            nc.sync.dma_start(out_rows[:, t : t + 2, halves[h]], res[h][:, t : t + 2, :])
+        def store_row_tile(t):
+            nc.sync.dma_start(out_rows[:, t, :].rearrange("p (h c) -> p h c", h=2), res[:, :, t, :])
 
+        all_columns = slice(0, S)
+        both = slice(0, 2)
         whole = slice(0, HALF)
         parts = [slice(0, HALF // 2), slice(HALF // 2, HALF)]
 
         for t in range(PACK):
             fetch_adv(t)
 
-        fetch_old(0)
-        for t in range(2):
-            fetch_old(t + 1)
-            for h in range(2):
-                product(t, h)
-            for h in range(2):
-                smaller(t, h, whole)
-        for h in range(2):
-            store_pair(0, h)
-        fetch_old(3)
+        fetch_old(0, [all_columns])
+        fetch_old(1, [all_columns])
+        product(0, all_columns)
+        fetch_old(2, [all_columns])
+        smaller(0, both, whole)
+        store_row_tile(0)
+        product(1, all_columns)
+        fetch_old(3, halves)
+        smaller(1, both, whole)
+        store_row_tile(1)
 
         for h, pieces in ((0, [whole]), (1, parts)):
-            for t in (2, 3):
-                product(t, h)
+            for t in range(2, PACK):
+                product(t, halves[h])
             for part in pieces:
-                for t in (2, 3):
+                for t in range(2, PACK):
                     smaller(t, h, part)
-            store_pair(2, h)
+            nc.sync.dma_start(out_rows[:, 2:PACK, halves[h]], res[:, h, 2:PACK, :])
 
         res_bf = tiles("res_bf", 2, [P, HALF, PACK], BF16)
         codes = tiles("codes", 2, [P, HALF], U32)
@@ -180,7 +183,7 @@ def tile_picked_ppo8_none_po_kernel(tc, x_words, x_scales, w1, old, adv, offs, s
         def round_and_weave(copy, h, part):
             copy(
                 res_bf[h][:, part, :].rearrange("p (c i) t -> p c t i", i=LINE),
-                res[h][:, :, part].rearrange("p t (c i) -> p c t i", i=LINE),
+                res[:, h, :, part].rearrange("p t (c i) -> p c t i", i=LINE),
             )
 
         round_and_weave(nc.scalar.copy, 0, whole)

@@ -71,7 +71,15 @@ def tile_picked_ppo8_none_po_kernel(tc, x_words, x_scales, w1, old, adv, offs, s
         for t in range(PACK):
             nc.sync.dma_start(old_sb[t][:], old_rows[:, t, :])
 
-        y = tiles("y", PACK, [P, S], F32)
+        last = PACK - 1
+        res = sb.tile([P, 2, PACK, HALF], F32, name="res", align_bytes=64)
+
+        def by_halves(ap):
+            return ap.rearrange("p (h c) -> p h c", h=2)
+
+        res_a = res[:, 0, :, :].rearrange("p t c -> p (t c)")
+        y = [by_halves(x[:]) for x in tiles("y", last, [P, S], F32)]
+        y = y + [by_halves(res_a[:, HALF // 2 : 7 * HALF // 2])[:, :, 0:HALF]]
         a = tiles("a", PACK, [P, S], F32)
         low_t = [w_raw[:, 0, :], w_raw[:, 2, :]] + [x[:] for x in tiles("low_t", 2, [P, S], F32)]
         rise_t = [w_raw[:, 1, :], w_raw[:, 3, :]] + [x[:] for x in tiles("rise_t", 2, [P, S], F32)]
@@ -106,7 +114,8 @@ def tile_picked_ppo8_none_po_kernel(tc, x_words, x_scales, w1, old, adv, offs, s
 
         first_bank = psum.tile([P, S], F32, name="first_bank")
 
-        def project(t, bank, picked):
+        def project(t, bank, h):
+            picked = slice(h.start * HALF, h.stop * HALF)
             cols = slice(t * P, (t + 1) * P)
             nc.tensor.matmul_mx(
                 out=bank[:, picked],
@@ -117,33 +126,30 @@ def tile_picked_ppo8_none_po_kernel(tc, x_words, x_scales, w1, old, adv, offs, s
                 start=True,
                 stop=True,
             )
-            nc.scalar.copy(y[t][:, picked], bank[:, picked])
+            nc.scalar.copy(y[t][:, h, :], by_halves(bank[:])[:, h, :])
 
-        project(0, first_bank, halves[0])
-        project(0, cap[0], halves[1])
+        project(0, first_bank, slice(0, 1))
+        project(0, cap[0], slice(1, 2))
         for t in range(1, PACK):
-            project(t, cap[t], slice(0, S))
+            project(t, cap[t], slice(0, 2))
 
         diff = tiles("diff", PACK, [P, S], F32)
         ratio = tiles("ratio", PACK, [P, S], F32)
-        plain = tiles("plain", PACK, [P, S], F32)
-        res = sb.tile([P, 2, PACK, HALF], F32, name="res", align_bytes=64)
+        plain = tiles("plain", last, [P, S], F32)
 
         def fetch_old(t, pieces):
             for cols in pieces:
                 entries = slice(cols.start // GROUP, cols.stop // GROUP)
-                nc.vector.tensor_tensor(diff[t][:, cols], old_sb[t][:].indirect(st_sb[:, entries]), y[t][:, cols], ALU.subtract)
+                y_part = y[t][:, cols.start // HALF, :] if t == last else y[t].rearrange("p h c -> p (h c)")
+                nc.vector.tensor_tensor(diff[t][:, cols], old_sb[t][:].indirect(st_sb[:, entries]), y_part, ALU.subtract)
             for cols in pieces:
                 nc.scalar.activation(ratio[t][:, cols], diff[t][:, cols], ACT.Exp, scale=-RATIO_SCALE)
 
-        def product(t, cols):
-            nc.vector.tensor_tensor(plain[t][:, cols], ratio[t][:, cols], a[t][:, cols], ALU.mult)
-
-        def by_halves(tile):
-            return tile[:].rearrange("p (h c) -> p h c", h=2)
+        def product(engine, t, cols):
+            engine.tensor_tensor(plain[t][:, cols], ratio[t][:, cols], a[t][:, cols], ALU.mult)
 
         def smaller(t, h, part):
-            nc.vector.tensor_tensor(res[:, h, t, part], by_halves(cap[t])[:, h, part], by_halves(plain[t])[:, h, part], ALU.min)
+            nc.vector.tensor_tensor(res[:, h, t, part], by_halves(cap[t][:])[:, h, part], by_halves(plain[t][:])[:, h, part], ALU.min)
 
         def store_row_tile(t):
             nc.sync.dma_start(out_rows[:, t, :].rearrange("p (h c) -> p h c", h=2), res[:, :, t, :])
@@ -158,21 +164,21 @@ def tile_picked_ppo8_none_po_kernel(tc, x_words, x_scales, w1, old, adv, offs, s
 
         fetch_old(0, [all_columns])
         fetch_old(1, [all_columns])
-        product(0, all_columns)
+        product(nc.vector, 0, all_columns)
         fetch_old(2, [all_columns])
-        smaller(0, both, whole)
-        store_row_tile(0)
-        product(1, all_columns)
-        fetch_old(3, halves)
-        smaller(1, both, whole)
-        store_row_tile(1)
-
+        product(nc.vector, 1, all_columns)
+        fetch_old(last, halves)
+        product(nc.vector, 2, all_columns)
+        plain = plain + [sb.tile([P, S], F32, name="old_sb3", align_bytes=64)]
+        for h in range(2):
+            product(nc.gpsimd, last, halves[h])
+        for t in range(2):
+            smaller(t, both, whole)
+            store_row_tile(t)
         for h, pieces in ((0, [whole]), (1, parts)):
-            for t in range(2, PACK):
-                product(t, halves[h])
+            smaller(2, h, whole)
             for part in pieces:
-                for t in range(2, PACK):
-                    smaller(t, h, part)
+                smaller(last, h, part)
             nc.sync.dma_start(out_rows[:, 2:PACK, halves[h]], res[:, h, 2:PACK, :])
 
         res_bf = tiles("res_bf", 2, [P, HALF, PACK], BF16)

@@ -22,7 +22,7 @@ QUADRANT = 32
 GROUP = 16
 HALF = S // 2
 LINE = 4
-A_T_BANKS = 3
+A_T_BANKS = 2
 CLIP_LO, CLIP_HI = 0.8, 1.25
 RATIO_SCALE = 0.25
 
@@ -77,17 +77,19 @@ def tile_picked_ppo8_none_po_kernel(tc, x_words, x_scales, w1, old, adv, offs, s
         def by_halves(ap):
             return ap.rearrange("p (h c) -> p h c", h=2)
 
-        res_a = res[:, 0, :, :].rearrange("p t c -> p (t c)")
-        y = [by_halves(x[:]) for x in tiles("y", last, [P, S], F32)]
-        y = y + [by_halves(res_a[:, HALF // 2 : 7 * HALF // 2])[:, :, 0:HALF]]
+        first_plain = sb.tile([P, 2, S], F32, name="first_plain", align_bytes=64)
+        y = [by_halves(x[:]) for x in tiles("y", last, [P, S], F32)] + [first_plain[:, :, 0:HALF]]
         a = tiles("a", PACK, [P, S], F32)
-        low_t = [w_raw[:, 0, :], w_raw[:, 2, :]] + [x[:] for x in tiles("low_t", 2, [P, S], F32)]
-        rise_t = [w_raw[:, 1, :], w_raw[:, 3, :]] + [x[:] for x in tiles("rise_t", 2, [P, S], F32)]
+        low_t = [x[:] for x in tiles("low_t", PACK, [P, S], F32)]
+        rise_t = [x[:] for x in tiles("rise_t", PACK, [P, S], F32)]
         cap = [psum.tile([P, S], F32, name="cap%d" % t) for t in range(PACK)]
+        low = [psum.tile([P, S], F32, name="low%d" % t) for t in range(2)]
         blocks = [slice(c * P, (c + 1) * P) for c in range(S // P)]
 
         def fetch_adv(t):
             nc.vector.tensor_copy(a[t][:], adv_sb[t][:].indirect(st_sb[:]))
+
+        def make_cap(t):
             a_t = psum.tile([P, S], F32, name="a_t", bufs=A_T_BANKS)
             for b in blocks:
                 nc.tensor.transpose(a_t[:, b], a[t][:, b], ident[:])
@@ -96,23 +98,23 @@ def tile_picked_ppo8_none_po_kernel(tc, x_words, x_scales, w1, old, adv, offs, s
             for b in blocks:
                 nc.tensor.matmul(cap[t][:, b], low_t[t][:, b], ident[:], start=True, stop=False, is_transpose=True)
                 nc.tensor.matmul(cap[t][:, b], rise_t[t][:, b], ident[:], start=False, stop=True, is_transpose=True)
+            if t < 2:
+                for b in blocks:
+                    nc.tensor.transpose(low[t][:, b], low_t[t][:, b], ident[:])
 
         xg_scales = sb.tile([P, S], U8, name="xg_scales", align_bytes=64)
         xg_words = sb.tile([P, S], U32, name="xg_words", align_bytes=64)
         nc.vector.tensor_copy(xg_scales[:], xs[:].indirect(offs_sb[:]))
 
         w_bf = sb.tile([P, PACK * N], BF16, name="w_bf", align_bytes=64)
-        w_dealt = w_bf[:].rearrange("p (t m j) -> p t m j", t=PACK, j=PACK)
-        w_plain = w_raw[:].rearrange("p j (m t) -> p t m j", t=PACK)
-        nc.vector.tensor_copy(w_dealt[:, :, 0 : P // 2, :], w_plain[:, :, 0 : P // 2, :])
-        nc.scalar.copy(w_dealt[:, :, P // 2 : P, :], w_plain[:, :, P // 2 : P, :])
+        w_dealt = w_bf[:].rearrange("p (t m j) -> p m j t", t=PACK, j=PACK)
+        w_plain = w_raw[:].rearrange("p j (m t) -> p m j t", t=PACK)
+        nc.vector.tensor_copy(w_dealt, w_plain)
         w_codes = sb.tile([P, N], U32, name="w_codes", align_bytes=64)
         w_scales = sb.tile([P, N], U8, name="w_scales", align_bytes=64)
         nc.vector.quantize_mx(out=w_codes[:].bitcast(FP8X4), scales=w_scales[:], in_=w_bf[:])
-        for h in range(2):
-            nc.vector.tensor_copy(xg_words[:, halves[h]], xw[:].indirect(offs_sb[:, list_halves[h]]))
+        nc.vector.tensor_copy(xg_words[:], xw[:].indirect(offs_sb[:]))
 
-        first_bank = psum.tile([P, S], F32, name="first_bank")
 
         def project(t, bank, h):
             picked = slice(h.start * HALF, h.stop * HALF)
@@ -128,14 +130,11 @@ def tile_picked_ppo8_none_po_kernel(tc, x_words, x_scales, w1, old, adv, offs, s
             )
             nc.scalar.copy(y[t][:, h, :], by_halves(bank[:])[:, h, :])
 
-        project(0, first_bank, slice(0, 1))
-        project(0, cap[0], slice(1, 2))
-        for t in range(1, PACK):
+        for t in range(PACK):
             project(t, cap[t], slice(0, 2))
 
         diff = tiles("diff", PACK, [P, S], F32)
         ratio = tiles("ratio", PACK, [P, S], F32)
-        plain = tiles("plain", last, [P, S], F32)
 
         def fetch_old(t, pieces):
             for cols in pieces:
@@ -149,7 +148,7 @@ def tile_picked_ppo8_none_po_kernel(tc, x_words, x_scales, w1, old, adv, offs, s
             engine.tensor_tensor(plain[t][:, cols], ratio[t][:, cols], a[t][:, cols], ALU.mult)
 
         def smaller(t, h, part):
-            nc.vector.tensor_tensor(res[:, h, t, part], by_halves(cap[t][:])[:, h, part], by_halves(plain[t][:])[:, h, part], ALU.min)
+            nc.vector.tensor_tensor(res[:, h, t, part], by_halves(cap[t][:])[:, h, part], by_halves(plain[t])[:, h, part], ALU.min)
 
         def store_row_tile(t):
             nc.sync.dma_start(out_rows[:, t, :].rearrange("p (h c) -> p h c", h=2), res[:, :, t, :])
@@ -161,17 +160,20 @@ def tile_picked_ppo8_none_po_kernel(tc, x_words, x_scales, w1, old, adv, offs, s
 
         for t in range(PACK):
             fetch_adv(t)
+            if t < last:
+                make_cap(t)
 
-        fetch_old(0, [all_columns])
-        fetch_old(1, [all_columns])
-        product(nc.vector, 0, all_columns)
-        fetch_old(2, [all_columns])
-        product(nc.vector, 1, all_columns)
+        for t in range(last):
+            fetch_old(t, [all_columns])
         fetch_old(last, halves)
-        product(nc.vector, 2, all_columns)
-        plain = plain + [sb.tile([P, S], F32, name="old_sb3", align_bytes=64)]
+        make_cap(last)
+        late_plain = sb.tile([P, 2, S], F32, name="old_sb3", align_bytes=64)
+        plain = [first_plain[:, 0, :], first_plain[:, 1, :], late_plain[:, 0, :], late_plain[:, 1, :]]
+        for t in range(2):
+            nc.vector.scalar_tensor_tensor(plain[t], low[t][:], 1.0 / CLIP_LO, ratio[t][:], ALU.mult, ALU.mult)
         for h in range(2):
-            product(nc.gpsimd, last, halves[h])
+            for t in range(2, PACK):
+                product(nc.gpsimd, t, halves[h])
         for t in range(2):
             smaller(t, both, whole)
             store_row_tile(t)

@@ -89,12 +89,14 @@ def tile_picked_ppo8_none_po_kernel(tc, x_words, x_scales, w1, old, adv, offs, s
         def fetch_adv(t):
             nc.vector.tensor_copy(a[t][:], adv_sb[t][:].indirect(st_sb[:]))
 
-        def make_cap(t):
+        def make_cap_terms(t):
             a_t = psum.tile([P, S], F32, name="a_t", bufs=A_T_BANKS)
             for b in blocks:
                 nc.tensor.transpose(a_t[:, b], a[t][:, b], ident[:])
             nc.scalar.activation(low_t[t], a_t[:], ACT.Copy, scale=CLIP_LO)
             nc.scalar.activation(rise_t[t], a_t[:], ACT.Relu, scale=CLIP_HI - CLIP_LO)
+
+        def make_cap(t):
             for b in blocks:
                 nc.tensor.matmul(cap[t][:, b], low_t[t][:, b], ident[:], start=True, stop=False, is_transpose=True)
                 nc.tensor.matmul(cap[t][:, b], rise_t[t][:, b], ident[:], start=False, stop=True, is_transpose=True)
@@ -113,7 +115,8 @@ def tile_picked_ppo8_none_po_kernel(tc, x_words, x_scales, w1, old, adv, offs, s
         w_codes = sb.tile([P, N], U32, name="w_codes", align_bytes=64)
         w_scales = sb.tile([P, N], U8, name="w_scales", align_bytes=64)
         nc.vector.quantize_mx(out=w_codes[:].bitcast(FP8X4), scales=w_scales[:], in_=w_bf[:])
-        nc.vector.tensor_copy(xg_words[:], xw[:].indirect(offs_sb[:]))
+        for h in range(2):
+            nc.vector.tensor_copy(xg_words[:, halves[h]], xw[:].indirect(offs_sb[:, list_halves[h]]))
 
 
         def project(t, bank, h):
@@ -130,7 +133,12 @@ def tile_picked_ppo8_none_po_kernel(tc, x_words, x_scales, w1, old, adv, offs, s
             )
             nc.scalar.copy(y[t][:, h, :], by_halves(bank[:])[:, h, :])
 
-        for t in range(PACK):
+        for t in range(2):
+            fetch_adv(t)
+            make_cap_terms(t)
+        project(0, psum.tile([P, S], F32, name="a_t", bufs=A_T_BANKS), slice(0, 1))
+        project(0, cap[0], slice(1, 2))
+        for t in range(1, PACK):
             project(t, cap[t], slice(0, 2))
 
         diff = tiles("diff", PACK, [P, S], F32)
@@ -158,22 +166,25 @@ def tile_picked_ppo8_none_po_kernel(tc, x_words, x_scales, w1, old, adv, offs, s
         whole = slice(0, HALF)
         parts = [slice(0, HALF // 2), slice(HALF // 2, HALF)]
 
-        for t in range(PACK):
+        for t in range(2):
+            make_cap(t)
+        for t in range(2, PACK):
             fetch_adv(t)
-            if t < last:
-                make_cap(t)
+        make_cap_terms(2)
+        make_cap(2)
 
         for t in range(last):
             fetch_old(t, [all_columns])
         fetch_old(last, halves)
+        make_cap_terms(last)
         make_cap(last)
         late_plain = sb.tile([P, 2, S], F32, name="old_sb3", align_bytes=64)
         plain = [first_plain[:, 0, :], first_plain[:, 1, :], late_plain[:, 0, :], late_plain[:, 1, :]]
         for t in range(2):
             nc.vector.scalar_tensor_tensor(plain[t], low[t][:], 1.0 / CLIP_LO, ratio[t][:], ALU.mult, ALU.mult)
+        product(nc.gpsimd, 2, all_columns)
         for h in range(2):
-            for t in range(2, PACK):
-                product(nc.gpsimd, t, halves[h])
+            product(nc.gpsimd, last, halves[h])
         for t in range(2):
             smaller(t, both, whole)
             store_row_tile(t)

@@ -25,6 +25,7 @@ LINE = 4
 A_T_BANKS = 2
 CLIP_LO, CLIP_HI = 0.8, 1.25
 RATIO_SCALE = 0.25
+W_SPLIT = 96
 
 
 def tile_picked_ppo8_none_po_kernel(tc, x_words, x_scales, w1, old, adv, offs, st, out_0, out_1, out_2):
@@ -79,7 +80,8 @@ def tile_picked_ppo8_none_po_kernel(tc, x_words, x_scales, w1, old, adv, offs, s
 
         first_plain = sb.tile([P, 2, S], F32, name="first_plain", align_bytes=64)
         y = [by_halves(x[:]) for x in tiles("y", last, [P, S], F32)] + [first_plain[:, :, 0:HALF]]
-        a = tiles("a", PACK, [P, S], F32)
+        late_a = sb.tile([P, 2 * S], F32, name="late_a", align_bytes=64)
+        a = [x[:] for x in tiles("a", 2, [P, S], F32)] + [late_a[:, 0:S], late_a[:, S : 2 * S]]
         low_t = [x[:] for x in tiles("low_t", PACK, [P, S], F32)]
         rise_t = [x[:] for x in tiles("rise_t", PACK, [P, S], F32)]
         cap = [psum.tile([P, S], F32, name="cap%d" % t) for t in range(PACK)]
@@ -87,7 +89,7 @@ def tile_picked_ppo8_none_po_kernel(tc, x_words, x_scales, w1, old, adv, offs, s
         blocks = [slice(c * P, (c + 1) * P) for c in range(S // P)]
 
         def fetch_adv(t):
-            nc.vector.tensor_copy(a[t][:], adv_sb[t][:].indirect(st_sb[:]))
+            nc.vector.tensor_copy(a[t], adv_sb[t][:].indirect(st_sb[:]))
 
         def make_cap_terms(t):
             a_t = psum.tile([P, S], F32, name="a_t", bufs=A_T_BANKS)
@@ -111,7 +113,11 @@ def tile_picked_ppo8_none_po_kernel(tc, x_words, x_scales, w1, old, adv, offs, s
         w_bf = sb.tile([P, PACK * N], BF16, name="w_bf", align_bytes=64)
         w_dealt = w_bf[:].rearrange("p (t m j) -> p m j t", t=PACK, j=PACK)
         w_plain = w_raw[:].rearrange("p j (m t) -> p m j t", t=PACK)
-        nc.vector.tensor_copy(w_dealt, w_plain)
+        nc.vector.tensor_copy(w_dealt[:, 0:W_SPLIT], w_plain[:, 0:W_SPLIT])
+        nc.scalar.copy(
+            w_dealt[:, W_SPLIT:P].rearrange("p m j t -> p t m j"),
+            w_plain[:, W_SPLIT:P].rearrange("p m j t -> p t m j"),
+        )
         w_codes = sb.tile([P, N], U32, name="w_codes", align_bytes=64)
         w_scales = sb.tile([P, N], U8, name="w_scales", align_bytes=64)
         nc.vector.quantize_mx(out=w_codes[:].bitcast(FP8X4), scales=w_scales[:], in_=w_bf[:])
@@ -136,13 +142,15 @@ def tile_picked_ppo8_none_po_kernel(tc, x_words, x_scales, w1, old, adv, offs, s
         for t in range(2):
             fetch_adv(t)
             make_cap_terms(t)
+        make_cap(0)
         project(0, psum.tile([P, S], F32, name="a_t", bufs=A_T_BANKS), slice(0, 1))
-        project(0, cap[0], slice(1, 2))
-        for t in range(1, PACK):
-            project(t, cap[t], slice(0, 2))
+        project(0, cap[2], slice(1, 2))
+        for t, bank in ((1, cap[1]), (2, cap[3]), (3, low[1])):
+            project(t, bank, slice(0, 2))
 
         diff = tiles("diff", PACK, [P, S], F32)
-        ratio = tiles("ratio", PACK, [P, S], F32)
+        late_ratio = sb.tile([P, 2 * S], F32, name="late_ratio", align_bytes=64)
+        ratio = [x[:] for x in tiles("ratio", 2, [P, S], F32)] + [late_ratio[:, 0:S], late_ratio[:, S : 2 * S]]
 
         def fetch_old(t, pieces):
             for cols in pieces:
@@ -151,9 +159,6 @@ def tile_picked_ppo8_none_po_kernel(tc, x_words, x_scales, w1, old, adv, offs, s
                 nc.vector.tensor_tensor(diff[t][:, cols], old_sb[t][:].indirect(st_sb[:, entries]), y_part, ALU.subtract)
             for cols in pieces:
                 nc.scalar.activation(ratio[t][:, cols], diff[t][:, cols], ACT.Exp, scale=-RATIO_SCALE)
-
-        def product(engine, t, cols):
-            engine.tensor_tensor(plain[t][:, cols], ratio[t][:, cols], a[t][:, cols], ALU.mult)
 
         def smaller(t, h, part):
             nc.vector.tensor_tensor(res[:, h, t, part], by_halves(cap[t][:])[:, h, part], by_halves(plain[t])[:, h, part], ALU.min)
@@ -166,25 +171,22 @@ def tile_picked_ppo8_none_po_kernel(tc, x_words, x_scales, w1, old, adv, offs, s
         whole = slice(0, HALF)
         parts = [slice(0, HALF // 2), slice(HALF // 2, HALF)]
 
-        for t in range(2):
-            make_cap(t)
         for t in range(2, PACK):
             fetch_adv(t)
         make_cap_terms(2)
-        make_cap(2)
 
         for t in range(last):
             fetch_old(t, [all_columns])
         fetch_old(last, halves)
         make_cap_terms(last)
-        make_cap(last)
-        late_plain = sb.tile([P, 2, S], F32, name="old_sb3", align_bytes=64)
-        plain = [first_plain[:, 0, :], first_plain[:, 1, :], late_plain[:, 0, :], late_plain[:, 1, :]]
+        for t in range(1, PACK):
+            make_cap(t)
+        late_plain = sb.tile([P, 2 * S], F32, name="old_sb3", align_bytes=64)
+        plain = [first_plain[:, 0, :], first_plain[:, 1, :], late_plain[:, 0:S], late_plain[:, S : 2 * S]]
         for t in range(2):
-            nc.vector.scalar_tensor_tensor(plain[t], low[t][:], 1.0 / CLIP_LO, ratio[t][:], ALU.mult, ALU.mult)
-        product(nc.gpsimd, 2, all_columns)
-        for h in range(2):
-            product(nc.gpsimd, last, halves[h])
+            nc.vector.scalar_tensor_tensor(plain[t], low[t][:], 1.0 / CLIP_LO, ratio[t], ALU.mult, ALU.mult)
+        for cols in (slice(0, S + HALF), slice(S + HALF, 2 * S)):
+            nc.gpsimd.tensor_tensor(late_plain[:, cols], late_ratio[:, cols], late_a[:, cols], ALU.mult)
         for t in range(2):
             smaller(t, both, whole)
             store_row_tile(t)

@@ -79,13 +79,13 @@ def tile_picked_ppo8_none_po_kernel(tc, x_words, x_scales, w1, old, adv, offs, s
             return ap.rearrange("p (h c) -> p h c", h=2)
 
         first_plain = sb.tile([P, 2, S], F32, name="first_plain", align_bytes=64)
-        y = [by_halves(x[:]) for x in tiles("y", last, [P, S], F32)] + [first_plain[:, :, 0:HALF]]
+        y = [by_halves(x[:]) for x in tiles("y", last, [P, S], F32)] + [by_halves(first_plain[:, 0, :])]
         late_a = sb.tile([P, 2 * S], F32, name="late_a", align_bytes=64)
         a = [x[:] for x in tiles("a", 2, [P, S], F32)] + [late_a[:, 0:S], late_a[:, S : 2 * S]]
         low_t = [x[:] for x in tiles("low_t", PACK, [P, S], F32)]
         rise_t = [x[:] for x in tiles("rise_t", PACK, [P, S], F32)]
-        cap = [psum.tile([P, S], F32, name="cap%d" % t) for t in range(PACK)]
-        low = [psum.tile([P, S], F32, name="low%d" % t) for t in range(2)]
+        cap = [[psum.tile([P, 2, HALF], F32, name="cap%d%d" % (pair, h)) for h in range(2)] for pair in range(2)]
+        low = [psum.tile([P, 2, HALF], F32, name="low%d" % h) for h in range(2)]
         blocks = [slice(c * P, (c + 1) * P) for c in range(S // P)]
 
         def fetch_adv(t):
@@ -98,13 +98,21 @@ def tile_picked_ppo8_none_po_kernel(tc, x_words, x_scales, w1, old, adv, offs, s
             nc.scalar.activation(low_t[t], a_t[:], ACT.Copy, scale=CLIP_LO)
             nc.scalar.activation(rise_t[t], a_t[:], ACT.Relu, scale=CLIP_HI - CLIP_LO)
 
-        def make_cap(t):
-            for b in blocks:
-                nc.tensor.matmul(cap[t][:, b], low_t[t][:, b], ident[:], start=True, stop=False, is_transpose=True)
-                nc.tensor.matmul(cap[t][:, b], rise_t[t][:, b], ident[:], start=False, stop=True, is_transpose=True)
-            if t < 2:
-                for b in blocks:
-                    nc.tensor.transpose(low[t][:, b], low_t[t][:, b], ident[:])
+        def half_blocks(h):
+            return [(slice(c * P, (c + 1) * P), slice(h * HALF + c * P, h * HALF + (c + 1) * P)) for c in range(HALF // P)]
+
+        def make_cap(pair, h):
+            for i in range(2):
+                t = 2 * pair + i
+                for place, b in half_blocks(h):
+                    out = cap[pair][h][:, i, place]
+                    nc.tensor.matmul(out, low_t[t][:, b], ident[:], start=True, stop=False, is_transpose=True)
+                    nc.tensor.matmul(out, rise_t[t][:, b], ident[:], start=False, stop=True, is_transpose=True)
+
+        def make_low(t):
+            for h in range(2):
+                for place, b in half_blocks(h):
+                    nc.tensor.transpose(low[h][:, t, place], low_t[t][:, b], ident[:])
 
         xg_scales = sb.tile([P, S], U8, name="xg_scales", align_bytes=64)
         xg_words = sb.tile([P, S], U32, name="xg_words", align_bytes=64)
@@ -137,20 +145,20 @@ def tile_picked_ppo8_none_po_kernel(tc, x_words, x_scales, w1, old, adv, offs, s
                 start=True,
                 stop=True,
             )
-            nc.scalar.copy(y[t][:, h, :], by_halves(bank[:])[:, h, :])
+            nc.scalar.copy(y[t][:, h, :], by_halves(bank)[:, h, :])
 
         for t in range(2):
             fetch_adv(t)
             make_cap_terms(t)
-        make_cap(0)
-        project(0, psum.tile([P, S], F32, name="a_t", bufs=A_T_BANKS), slice(0, 1))
-        project(0, cap[2], slice(1, 2))
-        for t, bank in ((1, cap[1]), (2, cap[3]), (3, low[1])):
-            project(t, bank, slice(0, 2))
+            make_low(t)
+        project(0, psum.tile([P, S], F32, name="a_t", bufs=A_T_BANKS)[:], slice(0, 1))
+        for t in range(PACK):
+            project(t, cap[t // 2][t % 2][:].rearrange("p i c -> p (i c)"), slice(1 if t == 0 else 0, 2))
 
         diff = tiles("diff", PACK, [P, S], F32)
-        late_ratio = sb.tile([P, 2 * S], F32, name="late_ratio", align_bytes=64)
-        ratio = [x[:] for x in tiles("ratio", 2, [P, S], F32)] + [late_ratio[:, 0:S], late_ratio[:, S : 2 * S]]
+        first_ratio = sb.tile([P, 2, S], F32, name="first_ratio", align_bytes=64)
+        late_ratio = res[:, 1, :, :].rearrange("p (h i) c -> p h i c", h=2)
+        ratio = [by_halves(first_ratio[:, i, :]) for i in range(2)] + [late_ratio[:, :, i, :] for i in range(2)]
 
         def fetch_old(t, pieces):
             for cols in pieces:
@@ -158,16 +166,10 @@ def tile_picked_ppo8_none_po_kernel(tc, x_words, x_scales, w1, old, adv, offs, s
                 y_part = y[t][:, cols.start // HALF, :] if t == last else y[t].rearrange("p h c -> p (h c)")
                 nc.vector.tensor_tensor(diff[t][:, cols], old_sb[t][:].indirect(st_sb[:, entries]), y_part, ALU.subtract)
             for cols in pieces:
-                nc.scalar.activation(ratio[t][:, cols], diff[t][:, cols], ACT.Exp, scale=-RATIO_SCALE)
-
-        def smaller(t, h, part):
-            nc.vector.tensor_tensor(res[:, h, t, part], by_halves(cap[t][:])[:, h, part], by_halves(plain[t])[:, h, part], ALU.min)
-
-        def store_row_tile(t):
-            nc.sync.dma_start(out_rows[:, t, :].rearrange("p (h c) -> p h c", h=2), res[:, :, t, :])
+                h = slice(cols.start // HALF, cols.stop // HALF)
+                nc.scalar.activation(ratio[t][:, h, :], by_halves(diff[t][:])[:, h, :], ACT.Exp, scale=-RATIO_SCALE)
 
         all_columns = slice(0, S)
-        both = slice(0, 2)
         whole = slice(0, HALF)
         parts = [slice(0, HALF // 2), slice(HALF // 2, HALF)]
 
@@ -179,22 +181,29 @@ def tile_picked_ppo8_none_po_kernel(tc, x_words, x_scales, w1, old, adv, offs, s
             fetch_old(t, [all_columns])
         fetch_old(last, halves)
         make_cap_terms(last)
-        for t in range(1, PACK):
-            make_cap(t)
-        late_plain = sb.tile([P, 2 * S], F32, name="old_sb3", align_bytes=64)
-        plain = [first_plain[:, 0, :], first_plain[:, 1, :], late_plain[:, 0:S], late_plain[:, S : 2 * S]]
-        for t in range(2):
-            nc.vector.scalar_tensor_tensor(plain[t], low[t][:], 1.0 / CLIP_LO, ratio[t], ALU.mult, ALU.mult)
-        for cols in (slice(0, S + HALF), slice(S + HALF, 2 * S)):
-            nc.gpsimd.tensor_tensor(late_plain[:, cols], late_ratio[:, cols], late_a[:, cols], ALU.mult)
-        for t in range(2):
-            smaller(t, both, whole)
-            store_row_tile(t)
-        for h, pieces in ((0, [whole]), (1, parts)):
-            smaller(2, h, whole)
-            for part in pieces:
-                smaller(last, h, part)
-            nc.sync.dma_start(out_rows[:, 2:PACK, halves[h]], res[:, h, 2:PACK, :])
+        for h in range(2):
+            for pair in range(2):
+                make_cap(pair, h)
+        late_plain = sb.tile([P, 2, S], F32, name="old_sb3", align_bytes=64)
+        plain = [first_plain, late_plain]
+        for h in range(2):
+            nc.vector.scalar_tensor_tensor(
+                first_plain[:, :, halves[h]], low[h][:], 1.0 / CLIP_LO, first_ratio[:, :, halves[h]], ALU.mult, ALU.mult
+            )
+        late_a_rows = late_a[:].rearrange("p (i c) -> p i c", i=2)
+        for h, part in ((0, whole), (1, parts[0]), (1, parts[1])):
+            nc.gpsimd.tensor_tensor(
+                late_plain[:, :, halves[h]][:, :, part], late_ratio[:, h, :, part], late_a_rows[:, :, halves[h]][:, :, part], ALU.mult
+            )
+
+        for h in range(2):
+            for pair in range(2):
+                rows = slice(2 * pair, 2 * pair + 2)
+                for part in parts if (h, pair) == (1, 1) else [whole]:
+                    nc.vector.tensor_tensor(
+                        res[:, h, rows, part], cap[pair][h][:, :, part], plain[pair][:, :, halves[h]][:, :, part], ALU.min
+                    )
+                nc.sync.dma_start(out_rows[:, rows, halves[h]], res[:, h, rows, :])
 
         res_bf = tiles("res_bf", 2, [P, HALF, PACK], BF16)
         codes = tiles("codes", 2, [P, HALF], U32)
@@ -208,8 +217,8 @@ def tile_picked_ppo8_none_po_kernel(tc, x_words, x_scales, w1, old, adv, offs, s
             )
 
         round_and_weave(nc.scalar.copy, 0, whole)
-        for part in parts:
-            round_and_weave(nc.vector.tensor_copy, 1, part)
+        round_and_weave(nc.vector.tensor_copy, 1, parts[1])
+        round_and_weave(nc.scalar.copy, 1, parts[0])
         for h in range(2):
             nc.vector.quantize_mx(
                 out=codes[h][:].bitcast(FP8X4),

@@ -20,6 +20,7 @@ P = 128
 PACK = 4
 QUADRANT = 32
 GROUP = 16
+SPREAD = 8
 HALF = S // 2
 LINE = 4
 A_T_BANKS = 2
@@ -45,8 +46,7 @@ def tile_picked_ppo8_none_po_kernel(tc, x_words, x_scales, w1, old, adv, offs, s
         xw = sb.tile([P, T], U32, name="xw", align_bytes=64)
         xs = sb.tile([P, T], U8, name="xs", align_bytes=64)
         w_raw = sb.tile([P, PACK, N], F32, name="w_raw", align_bytes=64)
-        adv_sb = tiles("adv_sb", PACK, [P, U], F32)
-        old_sb = tiles("old_sb", PACK, [P, U], F32)
+        adv_sb = tiles("adv_sb", 2, [P, U], F32)
 
         adv_rows = adv.rearrange("(p t) u -> p t u", t=PACK)
         old_rows = old.rearrange("(p t) u -> p t u", t=PACK)
@@ -62,15 +62,10 @@ def tile_picked_ppo8_none_po_kernel(tc, x_words, x_scales, w1, old, adv, offs, s
         nc.sync.dma_start(adv_sb[0][:], adv_rows[:, 0, :])
         nc.sync.dma_start(st_sb[:], st)
         nc.sync.dma_start(offs_sb[:], offs)
-        for r in range(PACK):
-            nc.sync.dma_start(xs[r:P:QUADRANT, :].bitcast(I32), x_scales[0].bitcast(I32)[r : K // 32 : PACK, :])
+        nc.sync.dma_start(xs[0:P:SPREAD, :].bitcast(I32), x_scales[0].bitcast(I32))
         nc.sync.dma_start(w_raw[:], w_rows)
         nc.sync.dma_start(adv_sb[1][:], adv_rows[:, 1, :])
         nc.sync.dma_start(xw[:].bitcast(I32), x_words[0].rearrange("p c r -> p (c r)").bitcast(I32))
-        nc.sync.dma_start(adv_sb[2][:], adv_rows[:, 2, :])
-        nc.sync.dma_start(adv_sb[3][:], adv_rows[:, 3, :])
-        for t in range(PACK):
-            nc.sync.dma_start(old_sb[t][:], old_rows[:, t, :])
 
         last = PACK - 1
         res = sb.tile([P, 2, PACK, HALF], F32, name="res", align_bytes=64)
@@ -90,6 +85,11 @@ def tile_picked_ppo8_none_po_kernel(tc, x_words, x_scales, w1, old, adv, offs, s
 
         def fetch_adv(t):
             nc.vector.tensor_copy(a[t], adv_sb[t][:].indirect(st_sb[:]))
+
+        def load_into_slot(slot, rows):
+            window = sb.tile([P, U], F32, name=slot, align_bytes=64)
+            nc.sync.dma_start(window[:], rows)
+            return window
 
         def make_cap_terms(t):
             a_t = psum.tile([P, S], F32, name="a_t", bufs=A_T_BANKS)
@@ -114,9 +114,16 @@ def tile_picked_ppo8_none_po_kernel(tc, x_words, x_scales, w1, old, adv, offs, s
                 for place, b in half_blocks(h):
                     nc.tensor.transpose(low[h][:, t, place], low_t[t][:, b], ident[:])
 
+        nc.scalar.activation(a[0], adv_sb[0][:].indirect(st_sb[:]), ACT.Copy)
+        picked_scales = sb.tile([P, S], U8, name="picked_scales", align_bytes=64)
         xg_scales = sb.tile([P, S], U8, name="xg_scales", align_bytes=64)
+        nc.gpsimd.memset(xg_scales[:].bitcast(I32), 0)
+        nc.vector.tensor_copy(picked_scales[:], xs[:].indirect(offs_sb[:]))
+        for r in range(PACK):
+            nc.scalar.dma_start(xg_scales[r:P:QUADRANT, :].bitcast(I32), picked_scales[SPREAD * r : P : QUADRANT, :].bitcast(I32))
+        adv_sb.append(load_into_slot("adv_sb0", adv_rows[:, 2, :]))
+        adv_sb.append(load_into_slot("xs", adv_rows[:, 3, :]))
         xg_words = sb.tile([P, S], U32, name="xg_words", align_bytes=64)
-        nc.vector.tensor_copy(xg_scales[:], xs[:].indirect(offs_sb[:]))
 
         w_bf = sb.tile([P, PACK * N], BF16, name="w_bf", align_bytes=64)
         w_dealt = w_bf[:].rearrange("p (t m j) -> p m j t", t=PACK, j=PACK)
@@ -147,10 +154,11 @@ def tile_picked_ppo8_none_po_kernel(tc, x_words, x_scales, w1, old, adv, offs, s
             )
             nc.scalar.copy(y[t][:, h, :], by_halves(bank)[:, h, :])
 
+        fetch_adv(1)
         for t in range(2):
-            fetch_adv(t)
             make_cap_terms(t)
             make_low(t)
+        old_sb = [load_into_slot(slot, old_rows[:, t, :]) for t, slot in enumerate(("w_raw", "adv_sb1", "w_bf", "xw"))]
         project(0, psum.tile([P, S], F32, name="a_t", bufs=A_T_BANKS)[:], slice(0, 1))
         for t in range(PACK):
             project(t, cap[t // 2][t % 2][:].rearrange("p i c -> p (i c)"), slice(1 if t == 0 else 0, 2))
@@ -184,7 +192,7 @@ def tile_picked_ppo8_none_po_kernel(tc, x_words, x_scales, w1, old, adv, offs, s
         for h in range(2):
             for pair in range(2):
                 make_cap(pair, h)
-        late_plain = sb.tile([P, 2, S], F32, name="old_sb3", align_bytes=64)
+        late_plain = sb.tile([P, 2, S], F32, name="xw", align_bytes=64)
         plain = [first_plain, late_plain]
         for h in range(2):
             nc.vector.scalar_tensor_tensor(

@@ -73,12 +73,19 @@ def tile_picked_ppo8_none_po_kernel(tc, x_words, x_scales, w1, old, adv, offs, s
         def by_halves(ap):
             return ap.rearrange("p (h c) -> p h c", h=2)
 
-        first_plain = sb.tile([P, 2, S], F32, name="first_plain", align_bytes=64)
-        y = [by_halves(x[:]) for x in tiles("y", last, [P, S], F32)] + [by_halves(first_plain[:, 0, :])]
+        plain = sb.tile([P, 2, PACK, HALF], F32, name="plain", align_bytes=64)
+        plain_a = plain[:, 0, :, :].rearrange("p t c -> p (t c)")
+        y = [by_halves(x[:]) for x in tiles("y", last, [P, S], F32)]
+        last_y = [plain_a[:, S - P : S + P], plain[:, 1, 0, :]]
         late_a = sb.tile([P, 2 * S], F32, name="late_a", align_bytes=64)
         a = [x[:] for x in tiles("a", 2, [P, S], F32)] + [late_a[:, 0:S], late_a[:, S : 2 * S]]
-        low_t = [x[:] for x in tiles("low_t", PACK, [P, S], F32)]
-        rise_t = [x[:] for x in tiles("rise_t", PACK, [P, S], F32)]
+        low_t = [x[:] for x in tiles("low_t", last, [P, S], F32)]
+        rise_t = [x[:] for x in tiles("rise_t", last, [P, S], F32)]
+        last_terms = tiles("last_terms", 2, [P, S], F32)
+        low_h = [[x[:, c] for c in halves] for x in low_t] + [[x[:, halves[0]] for x in last_terms]]
+        rise_h = [[x[:, c] for c in halves] for x in rise_t] + [[x[:, halves[1]] for x in last_terms]]
+        diff = [x[:] for x in tiles("diff", last, [P, S], F32)]
+        last_diff = [sb.tile([P, HALF], F32, name="last_diff", align_bytes=64)[:], last_terms[1][:, P : P + HALF]]
         cap = [[psum.tile([P, 2, HALF], F32, name="cap%d%d" % (pair, h)) for h in range(2)] for pair in range(2)]
         low = [psum.tile([P, 2, HALF], F32, name="low%d" % h) for h in range(2)]
         blocks = [slice(c * P, (c + 1) * P) for c in range(S // P)]
@@ -91,23 +98,27 @@ def tile_picked_ppo8_none_po_kernel(tc, x_words, x_scales, w1, old, adv, offs, s
             nc.sync.dma_start(window[:], rows)
             return window
 
-        def make_cap_terms(t):
+        def turn(t):
             a_t = psum.tile([P, S], F32, name="a_t", bufs=A_T_BANKS)
             for b in blocks:
                 nc.tensor.transpose(a_t[:, b], a[t][:, b], ident[:])
-            nc.scalar.activation(low_t[t], a_t[:], ACT.Copy, scale=CLIP_LO)
-            nc.scalar.activation(rise_t[t], a_t[:], ACT.Relu, scale=CLIP_HI - CLIP_LO)
+            return a_t
+
+        def make_terms(low_term, rise_term, a_t):
+            nc.scalar.activation(low_term, a_t, ACT.Copy, scale=CLIP_LO)
+            nc.scalar.activation(rise_term, a_t, ACT.Relu, scale=CLIP_HI - CLIP_LO)
+
+        def make_cap_terms(t):
+            make_terms(low_t[t], rise_t[t], turn(t)[:])
 
         def half_blocks(h):
             return [(slice(c * P, (c + 1) * P), slice(h * HALF + c * P, h * HALF + (c + 1) * P)) for c in range(HALF // P)]
 
-        def make_cap(pair, h):
-            for i in range(2):
-                t = 2 * pair + i
-                for place, b in half_blocks(h):
-                    out = cap[pair][h][:, i, place]
-                    nc.tensor.matmul(out, low_t[t][:, b], ident[:], start=True, stop=False, is_transpose=True)
-                    nc.tensor.matmul(out, rise_t[t][:, b], ident[:], start=False, stop=True, is_transpose=True)
+        def make_cap(t, h):
+            for place, b in half_blocks(h):
+                out = cap[t // 2][h][:, t % 2, place]
+                nc.tensor.matmul(out, low_h[t][h][:, place], ident[:], start=True, stop=False, is_transpose=True)
+                nc.tensor.matmul(out, rise_h[t][h][:, place], ident[:], start=False, stop=True, is_transpose=True)
 
         def make_low(t):
             for h in range(2):
@@ -152,7 +163,11 @@ def tile_picked_ppo8_none_po_kernel(tc, x_words, x_scales, w1, old, adv, offs, s
                 start=True,
                 stop=True,
             )
-            nc.scalar.copy(y[t][:, h, :], by_halves(bank)[:, h, :])
+            if t < last:
+                nc.scalar.copy(y[t][:, h, :], by_halves(bank)[:, h, :])
+            else:
+                for i in range(2):
+                    nc.scalar.copy(last_y[i], bank[:, halves[i]])
 
         fetch_adv(1)
         for t in range(2):
@@ -163,54 +178,54 @@ def tile_picked_ppo8_none_po_kernel(tc, x_words, x_scales, w1, old, adv, offs, s
         for t in range(PACK):
             project(t, cap[t // 2][t % 2][:].rearrange("p i c -> p (i c)"), slice(1 if t == 0 else 0, 2))
 
-        diff = tiles("diff", PACK, [P, S], F32)
         first_ratio = sb.tile([P, 2, S], F32, name="first_ratio", align_bytes=64)
         late_ratio = res[:, 1, :, :].rearrange("p (h i) c -> p h i c", h=2)
         ratio = [by_halves(first_ratio[:, i, :]) for i in range(2)] + [late_ratio[:, :, i, :] for i in range(2)]
 
-        def fetch_old(t, pieces):
-            for cols in pieces:
-                entries = slice(cols.start // GROUP, cols.stop // GROUP)
-                y_part = y[t][:, cols.start // HALF, :] if t == last else y[t].rearrange("p h c -> p (h c)")
-                nc.vector.tensor_tensor(diff[t][:, cols], old_sb[t][:].indirect(st_sb[:, entries]), y_part, ALU.subtract)
-            for cols in pieces:
-                h = slice(cols.start // HALF, cols.stop // HALF)
-                nc.scalar.activation(ratio[t][:, h, :], by_halves(diff[t][:])[:, h, :], ACT.Exp, scale=-RATIO_SCALE)
+        def fetch_old(t):
+            nc.vector.tensor_tensor(diff[t], old_sb[t][:].indirect(st_sb[:]), y[t].rearrange("p h c -> p (h c)"), ALU.subtract)
+            nc.scalar.activation(ratio[t], by_halves(diff[t]), ACT.Exp, scale=-RATIO_SCALE)
 
-        all_columns = slice(0, S)
+        def fetch_last_old(h):
+            window = old_sb[last][:].indirect(st_sb[:, list_halves[h]])
+            nc.vector.tensor_tensor(last_diff[h], window, last_y[h], ALU.subtract)
+            nc.scalar.activation(ratio[last][:, h, :], last_diff[h], ACT.Exp, scale=-RATIO_SCALE)
+
         whole = slice(0, HALF)
         parts = [slice(0, HALF // 2), slice(HALF // 2, HALF)]
 
         for t in range(2, PACK):
             fetch_adv(t)
         make_cap_terms(2)
-
+        last_a_t = turn(last)
         for t in range(last):
-            fetch_old(t, [all_columns])
-        fetch_old(last, halves)
-        make_cap_terms(last)
+            fetch_old(t)
         for h in range(2):
-            for pair in range(2):
-                make_cap(pair, h)
-        late_plain = sb.tile([P, 2, S], F32, name="xw", align_bytes=64)
-        plain = [first_plain, late_plain]
+            fetch_last_old(h)
+        for h in range(2):
+            make_terms(low_h[last][h], rise_h[last][h], last_a_t[:, halves[h]])
+        for h in range(2):
+            for t in range(PACK):
+                make_cap(t, h)
         for h in range(2):
             nc.vector.scalar_tensor_tensor(
-                first_plain[:, :, halves[h]], low[h][:], 1.0 / CLIP_LO, first_ratio[:, :, halves[h]], ALU.mult, ALU.mult
+                plain[:, h, 0:2, :], low[h][:], 1.0 / CLIP_LO, first_ratio[:, :, halves[h]], ALU.mult, ALU.mult
             )
         late_a_rows = late_a[:].rearrange("p (i c) -> p i c", i=2)
-        for h, part in ((0, whole), (1, parts[0]), (1, parts[1])):
+        both = slice(0, 2)
+        for rows, h, part in ((slice(0, 1), 0, whole), (slice(1, 2), 0, whole), (both, 1, parts[0]), (both, 1, parts[1])):
             nc.gpsimd.tensor_tensor(
-                late_plain[:, :, halves[h]][:, :, part], late_ratio[:, h, :, part], late_a_rows[:, :, halves[h]][:, :, part], ALU.mult
+                plain[:, h, 2:PACK, part][:, rows, :],
+                late_ratio[:, h, rows, part],
+                late_a_rows[:, rows, halves[h]][:, :, part],
+                ALU.mult,
             )
 
         for h in range(2):
             for pair in range(2):
                 rows = slice(2 * pair, 2 * pair + 2)
                 for part in parts if (h, pair) == (1, 1) else [whole]:
-                    nc.vector.tensor_tensor(
-                        res[:, h, rows, part], cap[pair][h][:, :, part], plain[pair][:, :, halves[h]][:, :, part], ALU.min
-                    )
+                    nc.vector.tensor_tensor(res[:, h, rows, part], cap[pair][h][:, :, part], plain[:, h, rows, part], ALU.min)
                 nc.sync.dma_start(out_rows[:, rows, halves[h]], res[:, h, rows, :])
 
         res_bf = tiles("res_bf", 2, [P, HALF, PACK], BF16)

@@ -75,17 +75,21 @@ def tile_picked_ppo8_none_po_kernel(tc, x_words, x_scales, w1, old, adv, offs, s
 
         plain = sb.tile([P, 2, PACK, HALF], F32, name="plain", align_bytes=64)
         plain_a = plain[:, 0, :, :].rearrange("p t c -> p (t c)")
-        y = [by_halves(x[:]) for x in tiles("y", last, [P, S], F32)]
         last_y = [plain_a[:, S - P : S + P], plain[:, 1, 0, :]]
-        late_a = sb.tile([P, 2 * S], F32, name="late_a", align_bytes=64)
-        a = [x[:] for x in tiles("a", 2, [P, S], F32)] + [late_a[:, 0:S], late_a[:, S : 2 * S]]
-        low_t = [x[:] for x in tiles("low_t", last, [P, S], F32)]
-        rise_t = [x[:] for x in tiles("rise_t", last, [P, S], F32)]
-        last_terms = tiles("last_terms", 2, [P, S], F32)
-        low_h = [[x[:, c] for c in halves] for x in low_t] + [[x[:, halves[0]] for x in last_terms]]
-        rise_h = [[x[:, c] for c in halves] for x in rise_t] + [[x[:, halves[1]] for x in last_terms]]
+        late = sb.tile([P, 6 * HALF], F32, name="late", align_bytes=64)
+
+        def piece(first_half):
+            return late[:, first_half * HALF : first_half * HALF + S]
+
+        late_a_rows = late[:].rearrange("p (i c) -> p i c", i=2)[:, :, 0:S]
+        a = [x[:] for x in tiles("a", 2, [P, S], F32)] + [piece(0), piece(3)]
+        y = [by_halves(x) for x in [piece(4)] + [x[:] for x in tiles("y", 2, [P, S], F32)]]
         diff = [x[:] for x in tiles("diff", last, [P, S], F32)]
-        last_diff = [sb.tile([P, HALF], F32, name="last_diff", align_bytes=64)[:], last_terms[1][:, P : P + HALF]]
+        low_t = [x[:] for x in tiles("low_t", 2, [P, S], F32)]
+        rise_t = [x[:] for x in tiles("rise_t", 2, [P, S], F32)]
+        a_terms = tiles("a_terms", 2, [P, S], F32)
+        b_terms = sb.tile([P, 2 * S], F32, name="b_terms", align_bytes=64)
+        last_diff = [b_terms[:, 0:HALF], b_terms[:, S : S + HALF]]
         cap = [[psum.tile([P, 2, HALF], F32, name="cap%d%d" % (pair, h)) for h in range(2)] for pair in range(2)]
         low = [psum.tile([P, 2, HALF], F32, name="low%d" % h) for h in range(2)]
         blocks = [slice(c * P, (c + 1) * P) for c in range(S // P)]
@@ -114,11 +118,24 @@ def tile_picked_ppo8_none_po_kernel(tc, x_words, x_scales, w1, old, adv, offs, s
         def half_blocks(h):
             return [(slice(c * P, (c + 1) * P), slice(h * HALF + c * P, h * HALF + (c + 1) * P)) for c in range(HALF // P)]
 
-        def make_cap(t, h):
-            for place, b in half_blocks(h):
-                out = cap[t // 2][h][:, t % 2, place]
-                nc.tensor.matmul(out, low_h[t][h][:, place], ident[:], start=True, stop=False, is_transpose=True)
-                nc.tensor.matmul(out, rise_h[t][h][:, place], ident[:], start=False, stop=True, is_transpose=True)
+        def add_back(bank, low_term, rise_term):
+            pieces = [slice(c, c + P) for c in range(0, bank.shape[1], P)]
+            for b in pieces:
+                nc.tensor.matmul(bank[:, b], low_term[:, b], ident[:], start=b == pieces[0], stop=False, is_transpose=True)
+            for b in pieces:
+                nc.tensor.matmul(bank[:, b], rise_term[:, b], ident[:], start=False, stop=b == pieces[-1], is_transpose=True)
+
+        def turn_half(tiles_turned, h):
+            a_t = psum.tile([P, S], F32, name="a_t", bufs=A_T_BANKS)
+            for i, t in enumerate(tiles_turned):
+                for place, b in half_blocks(h):
+                    nc.tensor.transpose(a_t[:, halves[i]][:, place], a[t][:, b], ident[:])
+            return a_t
+
+        def make_late_a_cap(i):
+            terms = [a_terms[i][:, c] for c in halves]
+            make_terms(terms[0], terms[1], turn_half([2 + i], 0)[:, halves[0]])
+            add_back(cap[1][0][:, i, :], terms[0], terms[1])
 
         def make_low(t):
             for h in range(2):
@@ -133,7 +150,7 @@ def tile_picked_ppo8_none_po_kernel(tc, x_words, x_scales, w1, old, adv, offs, s
         for r in range(PACK):
             nc.scalar.dma_start(xg_scales[r:P:QUADRANT, :].bitcast(I32), picked_scales[SPREAD * r : P : QUADRANT, :].bitcast(I32))
         adv_sb.append(load_into_slot("adv_sb0", adv_rows[:, 2, :]))
-        adv_sb.append(load_into_slot("xs", adv_rows[:, 3, :]))
+        adv_sb.append(load_into_slot("xs", adv_rows[:, last, :]))
         xg_words = sb.tile([P, S], U32, name="xg_words", align_bytes=64)
 
         w_bf = sb.tile([P, PACK * N], BF16, name="w_bf", align_bytes=64)
@@ -194,24 +211,27 @@ def tile_picked_ppo8_none_po_kernel(tc, x_words, x_scales, w1, old, adv, offs, s
         whole = slice(0, HALF)
         parts = [slice(0, HALF // 2), slice(HALF // 2, HALF)]
 
-        for t in range(2, PACK):
-            fetch_adv(t)
-        make_cap_terms(2)
-        last_a_t = turn(last)
-        for t in range(last):
+        fetch_adv(2)
+        nc.vector.tensor_copy(a[last][:, halves[0]], adv_sb[last][:].indirect(st_sb[:, list_halves[0]]))
+        for i in range(2):
+            make_late_a_cap(i)
+        for h in range(2):
+            for t in range(2):
+                add_back(cap[0][h][:, t, :], low_t[t][:, halves[h]], rise_t[t][:, halves[h]])
+        fetch_old(0)
+        nc.scalar.activation(a[last][:, halves[1]], adv_sb[last][:].indirect(st_sb[:, list_halves[1]]), ACT.Copy)
+        b_t = turn_half([2, last], 1)
+        for t in range(1, last):
             fetch_old(t)
-        for h in range(2):
-            fetch_last_old(h)
-        for h in range(2):
-            make_terms(low_h[last][h], rise_h[last][h], last_a_t[:, halves[h]])
-        for h in range(2):
-            for t in range(PACK):
-                make_cap(t, h)
+        fetch_last_old(0)
+        nc.scalar.activation(b_terms[:, 0:S], b_t[:], ACT.Copy, scale=CLIP_LO)
+        fetch_last_old(1)
+        nc.scalar.activation(b_terms[:, S : 2 * S], b_t[:], ACT.Relu, scale=CLIP_HI - CLIP_LO)
+        add_back(cap[1][1][:].rearrange("p i c -> p (i c)"), b_terms[:, 0:S], b_terms[:, S : 2 * S])
         for h in range(2):
             nc.vector.scalar_tensor_tensor(
                 plain[:, h, 0:2, :], low[h][:], 1.0 / CLIP_LO, first_ratio[:, :, halves[h]], ALU.mult, ALU.mult
             )
-        late_a_rows = late_a[:].rearrange("p (i c) -> p i c", i=2)
         both = slice(0, 2)
         for rows, h, part in ((slice(0, 1), 0, whole), (slice(1, 2), 0, whole), (both, 1, parts[0]), (both, 1, parts[1])):
             nc.gpsimd.tensor_tensor(

@@ -26,7 +26,6 @@ LINE = 4
 A_T_BANKS = 2
 CLIP_LO, CLIP_HI = 0.8, 1.25
 RATIO_SCALE = 0.25
-W_SPLIT = 96
 
 
 def tile_picked_ppo8_none_po_kernel(tc, x_words, x_scales, w1, old, adv, offs, st, out_0, out_1, out_2):
@@ -87,8 +86,7 @@ def tile_picked_ppo8_none_po_kernel(tc, x_words, x_scales, w1, old, adv, offs, s
         diff = [x[:] for x in tiles("diff", last, [P, S], F32)]
         low_t = [x[:] for x in tiles("low_t", 2, [P, S], F32)]
         rise_t = [x[:] for x in tiles("rise_t", 2, [P, S], F32)]
-        a_terms = tiles("a_terms", 2, [P, S], F32)
-        b_terms = sb.tile([P, 2 * S], F32, name="b_terms", align_bytes=64)
+        a_terms, b_terms = tiles("late_terms", 2, [P, 2 * S], F32)
         last_diff = [b_terms[:, 0:HALF], b_terms[:, S : S + HALF]]
         cap = [[psum.tile([P, 2, HALF], F32, name="cap%d%d" % (pair, h)) for h in range(2)] for pair in range(2)]
         low = [psum.tile([P, 2, HALF], F32, name="low%d" % h) for h in range(2)]
@@ -125,17 +123,12 @@ def tile_picked_ppo8_none_po_kernel(tc, x_words, x_scales, w1, old, adv, offs, s
             for b in pieces:
                 nc.tensor.matmul(bank[:, b], rise_term[:, b], ident[:], start=False, stop=b == pieces[-1], is_transpose=True)
 
-        def turn_half(tiles_turned, h):
+        def turn_late(h):
             a_t = psum.tile([P, S], F32, name="a_t", bufs=A_T_BANKS)
-            for i, t in enumerate(tiles_turned):
+            for i in range(2):
                 for place, b in half_blocks(h):
-                    nc.tensor.transpose(a_t[:, halves[i]][:, place], a[t][:, b], ident[:])
+                    nc.tensor.transpose(a_t[:, halves[i]][:, place], a[2 + i][:, b], ident[:])
             return a_t
-
-        def make_late_a_cap(i):
-            terms = [a_terms[i][:, c] for c in halves]
-            make_terms(terms[0], terms[1], turn_half([2 + i], 0)[:, halves[0]])
-            add_back(cap[1][0][:, i, :], terms[0], terms[1])
 
         def make_low(t):
             for h in range(2):
@@ -156,11 +149,7 @@ def tile_picked_ppo8_none_po_kernel(tc, x_words, x_scales, w1, old, adv, offs, s
         w_bf = sb.tile([P, PACK * N], BF16, name="w_bf", align_bytes=64)
         w_dealt = w_bf[:].rearrange("p (t m j) -> p m j t", t=PACK, j=PACK)
         w_plain = w_raw[:].rearrange("p j (m t) -> p m j t", t=PACK)
-        nc.vector.tensor_copy(w_dealt[:, 0:W_SPLIT], w_plain[:, 0:W_SPLIT])
-        nc.scalar.copy(
-            w_dealt[:, W_SPLIT:P].rearrange("p m j t -> p t m j"),
-            w_plain[:, W_SPLIT:P].rearrange("p m j t -> p t m j"),
-        )
+        nc.vector.tensor_copy(w_dealt, w_plain)
         w_codes = sb.tile([P, N], U32, name="w_codes", align_bytes=64)
         w_scales = sb.tile([P, N], U8, name="w_scales", align_bytes=64)
         nc.vector.quantize_mx(out=w_codes[:].bitcast(FP8X4), scales=w_scales[:], in_=w_bf[:])
@@ -213,14 +202,14 @@ def tile_picked_ppo8_none_po_kernel(tc, x_words, x_scales, w1, old, adv, offs, s
 
         fetch_adv(2)
         nc.vector.tensor_copy(a[last][:, halves[0]], adv_sb[last][:].indirect(st_sb[:, list_halves[0]]))
-        for i in range(2):
-            make_late_a_cap(i)
+        make_terms(a_terms[:, 0:S], a_terms[:, S : 2 * S], turn_late(0)[:])
+        add_back(cap[1][0][:].rearrange("p i c -> p (i c)"), a_terms[:, 0:S], a_terms[:, S : 2 * S])
         for h in range(2):
             for t in range(2):
                 add_back(cap[0][h][:, t, :], low_t[t][:, halves[h]], rise_t[t][:, halves[h]])
         fetch_old(0)
         nc.scalar.activation(a[last][:, halves[1]], adv_sb[last][:].indirect(st_sb[:, list_halves[1]]), ACT.Copy)
-        b_t = turn_half([2, last], 1)
+        b_t = turn_late(1)
         for t in range(1, last):
             fetch_old(t)
         fetch_last_old(0)

@@ -73,8 +73,6 @@ def tile_picked_ppo8_none_po_kernel(tc, x_words, x_scales, w1, old, adv, offs, s
             return ap.rearrange("p (h c) -> p h c", h=2)
 
         plain = sb.tile([P, 2, PACK, HALF], F32, name="plain", align_bytes=64)
-        plain_a = plain[:, 0, :, :].rearrange("p t c -> p (t c)")
-        last_y = [plain_a[:, S - P : S + P], plain[:, 1, 0, :]]
         late = sb.tile([P, 6 * HALF], F32, name="late", align_bytes=64)
 
         def piece(first_half):
@@ -82,7 +80,7 @@ def tile_picked_ppo8_none_po_kernel(tc, x_words, x_scales, w1, old, adv, offs, s
 
         late_a_rows = late[:].rearrange("p (i c) -> p i c", i=2)[:, :, 0:S]
         a = [x[:] for x in tiles("a", 2, [P, S], F32)] + [piece(0), piece(3)]
-        y = [by_halves(x) for x in [piece(4)] + [x[:] for x in tiles("y", 2, [P, S], F32)]]
+        y = [by_halves(x) for x in [piece(4)] + [x[:] for x in tiles("y", 2, [P, S], F32)]] + [plain[:, :, 0, :]]
         diff = [x[:] for x in tiles("diff", last, [P, S], F32)]
         low_t = [x[:] for x in tiles("low_t", 2, [P, S], F32)]
         rise_t = [x[:] for x in tiles("rise_t", 2, [P, S], F32)]
@@ -169,11 +167,7 @@ def tile_picked_ppo8_none_po_kernel(tc, x_words, x_scales, w1, old, adv, offs, s
                 start=True,
                 stop=True,
             )
-            if t < last:
-                nc.scalar.copy(y[t][:, h, :], by_halves(bank)[:, h, :])
-            else:
-                for i in range(2):
-                    nc.scalar.copy(last_y[i], bank[:, halves[i]])
+            nc.scalar.copy(y[t][:, h, :], by_halves(bank)[:, h, :])
 
         fetch_adv(1)
         for t in range(2):
@@ -194,7 +188,7 @@ def tile_picked_ppo8_none_po_kernel(tc, x_words, x_scales, w1, old, adv, offs, s
 
         def fetch_last_old(h):
             window = old_sb[last][:].indirect(st_sb[:, list_halves[h]])
-            nc.vector.tensor_tensor(last_diff[h], window, last_y[h], ALU.subtract)
+            nc.vector.tensor_tensor(last_diff[h], window, y[last][:, h, :], ALU.subtract)
             nc.scalar.activation(ratio[last][:, h, :], last_diff[h], ACT.Exp, scale=-RATIO_SCALE)
 
         whole = slice(0, HALF)
@@ -221,13 +215,9 @@ def tile_picked_ppo8_none_po_kernel(tc, x_words, x_scales, w1, old, adv, offs, s
             nc.vector.scalar_tensor_tensor(
                 plain[:, h, 0:2, :], low[h][:], 1.0 / CLIP_LO, first_ratio[:, :, halves[h]], ALU.mult, ALU.mult
             )
-        both = slice(0, 2)
-        for rows, h, part in ((slice(0, 1), 0, whole), (slice(1, 2), 0, whole), (both, 1, parts[0]), (both, 1, parts[1])):
+        for h, part in ((0, whole), (1, parts[0]), (1, parts[1])):
             nc.gpsimd.tensor_tensor(
-                plain[:, h, 2:PACK, part][:, rows, :],
-                late_ratio[:, h, rows, part],
-                late_a_rows[:, rows, halves[h]][:, :, part],
-                ALU.mult,
+                plain[:, h, 2:PACK, part], late_ratio[:, h, :, part], late_a_rows[:, :, halves[h]][:, :, part], ALU.mult
             )
 
         for h in range(2):

@@ -84,7 +84,8 @@ def tile_picked_ppo8_none_po_kernel(tc, x_words, x_scales, w1, old, adv, offs, s
         diff = [x[:] for x in tiles("diff", last, [P, S], F32)]
         low_t = [x[:] for x in tiles("low_t", 2, [P, S], F32)]
         rise_t = [x[:] for x in tiles("rise_t", 2, [P, S], F32)]
-        a_terms, b_terms = tiles("late_terms", 2, [P, 2 * S], F32)
+        a_terms = tiles("a_terms", 2, [P, S], F32)
+        b_terms = sb.tile([P, 2 * S], F32, name="b_terms", align_bytes=64)
         last_diff = [b_terms[:, 0:HALF], b_terms[:, S : S + HALF]]
         cap = [[psum.tile([P, 2, HALF], F32, name="cap%d%d" % (pair, h)) for h in range(2)] for pair in range(2)]
         low = [psum.tile([P, 2, HALF], F32, name="low%d" % h) for h in range(2)]
@@ -121,12 +122,17 @@ def tile_picked_ppo8_none_po_kernel(tc, x_words, x_scales, w1, old, adv, offs, s
             for b in pieces:
                 nc.tensor.matmul(bank[:, b], rise_term[:, b], ident[:], start=False, stop=b == pieces[-1], is_transpose=True)
 
-        def turn_late(h):
+        def turn_half(tiles_turned, h):
             a_t = psum.tile([P, S], F32, name="a_t", bufs=A_T_BANKS)
-            for i in range(2):
+            for i, t in enumerate(tiles_turned):
                 for place, b in half_blocks(h):
-                    nc.tensor.transpose(a_t[:, halves[i]][:, place], a[2 + i][:, b], ident[:])
+                    nc.tensor.transpose(a_t[:, halves[i]][:, place], a[t][:, b], ident[:])
             return a_t
+
+        def make_late_a_cap(i):
+            terms = [a_terms[i][:, c] for c in halves]
+            make_terms(terms[0], terms[1], turn_half([2 + i], 0)[:, halves[0]])
+            add_back(cap[1][0][:, i, :], terms[0], terms[1])
 
         def make_low(t):
             for h in range(2):
@@ -140,8 +146,7 @@ def tile_picked_ppo8_none_po_kernel(tc, x_words, x_scales, w1, old, adv, offs, s
         nc.vector.tensor_copy(picked_scales[:], xs[:].indirect(offs_sb[:]))
         for r in range(PACK):
             nc.scalar.dma_start(xg_scales[r:P:QUADRANT, :].bitcast(I32), picked_scales[SPREAD * r : P : QUADRANT, :].bitcast(I32))
-        adv_sb.append(load_into_slot("adv_sb0", adv_rows[:, 2, :]))
-        adv_sb.append(load_into_slot("xs", adv_rows[:, last, :]))
+        adv_sb.append(load_into_slot("xs", adv_rows[:, 2, :]))
         xg_words = sb.tile([P, S], U32, name="xg_words", align_bytes=64)
 
         w_bf = sb.tile([P, PACK * N], BF16, name="w_bf", align_bytes=64)
@@ -173,7 +178,8 @@ def tile_picked_ppo8_none_po_kernel(tc, x_words, x_scales, w1, old, adv, offs, s
         for t in range(2):
             make_cap_terms(t)
             make_low(t)
-        old_sb = [load_into_slot(slot, old_rows[:, t, :]) for t, slot in enumerate(("w_raw", "adv_sb1", "w_bf", "xw"))]
+        adv_sb.append(load_into_slot("w_raw", adv_rows[:, last, :]))
+        old_sb = [load_into_slot(slot, old_rows[:, t, :]) for t, slot in enumerate(("adv_sb1", "w_bf", "picked_scales", "xw"))]
         project(0, psum.tile([P, S], F32, name="a_t", bufs=A_T_BANKS)[:], slice(0, 1))
         for t in range(PACK):
             project(t, cap[t // 2][t % 2][:].rearrange("p i c -> p (i c)"), slice(1 if t == 0 else 0, 2))
@@ -196,14 +202,14 @@ def tile_picked_ppo8_none_po_kernel(tc, x_words, x_scales, w1, old, adv, offs, s
 
         fetch_adv(2)
         nc.vector.tensor_copy(a[last][:, halves[0]], adv_sb[last][:].indirect(st_sb[:, list_halves[0]]))
-        make_terms(a_terms[:, 0:S], a_terms[:, S : 2 * S], turn_late(0)[:])
-        add_back(cap[1][0][:].rearrange("p i c -> p (i c)"), a_terms[:, 0:S], a_terms[:, S : 2 * S])
+        for i in range(2):
+            make_late_a_cap(i)
         for h in range(2):
             for t in range(2):
                 add_back(cap[0][h][:, t, :], low_t[t][:, halves[h]], rise_t[t][:, halves[h]])
         fetch_old(0)
         nc.scalar.activation(a[last][:, halves[1]], adv_sb[last][:].indirect(st_sb[:, list_halves[1]]), ACT.Copy)
-        b_t = turn_late(1)
+        b_t = turn_half([2, last], 1)
         for t in range(1, last):
             fetch_old(t)
         fetch_last_old(0)

@@ -52,6 +52,9 @@ def tile_picked_ppo8_none_po_kernel(tc, x_words, x_scales, w1, old, adv, offs, s
         w_rows = w1.rearrange("(p j) c -> p j c", j=PACK)
         out_rows = out_0.rearrange("(p t) j -> p t j", t=PACK)
 
+        warm = sb.tile([P, 2], F32, name="warm")
+        nc.gpsimd.memset(warm[:, 0:1], 0.0)
+        nc.scalar.activation(warm[:, 1:2], warm[:, 0:1], ACT.Exp)
         xs_words = xs[:].bitcast(I32)
         nc.gpsimd.memset(xs_words[:, 0 : T // 8], 0)
         nc.vector.memset(xs_words[:, T // 8 : T // 4], 0)

@@ -44,7 +44,8 @@ def tile_picked_ppo8_none_po_kernel(tc, x_words, x_scales, w1, old, adv, offs, s
         st_sb = sb.tile([P, S // GROUP], U16, name="st_sb")
         xw = sb.tile([P, T], U32, name="xw", align_bytes=64)
         xs = sb.tile([P, T], U8, name="xs", align_bytes=64)
-        w_raw = sb.tile([P, PACK, N], F32, name="w_raw", align_bytes=64)
+        w_pool = ctx.enter_context(tc.tile_pool(name="w_pool", bufs=1))
+        w_raw = w_pool.tile([P, PACK, N], F32, name="w_raw", align_bytes=64, offset=0)
         adv_sb = tiles("adv_sb", 2, [P, U], F32)
 
         adv_rows = adv.rearrange("(p t) u -> p t u", t=PACK)
@@ -76,14 +77,8 @@ def tile_picked_ppo8_none_po_kernel(tc, x_words, x_scales, w1, old, adv, offs, s
             return ap.rearrange("p (h c) -> p h c", h=2)
 
         plain = sb.tile([P, 2, PACK, HALF], F32, name="plain", align_bytes=64)
-        late = sb.tile([P, 6 * HALF], F32, name="late", align_bytes=64)
-
-        def piece(first_half):
-            return late[:, first_half * HALF : first_half * HALF + S]
-
-        late_a_rows = late[:].rearrange("p (i c) -> p i c", i=2)[:, :, 0:S]
-        a = [x[:] for x in tiles("a", 2, [P, S], F32)] + [piece(0), piece(3)]
-        y = [by_halves(x) for x in [piece(4)] + [x[:] for x in tiles("y", 2, [P, S], F32)]] + [plain[:, :, 0, :]]
+        a = [sb.tile([P, S], F32, name="a", align_bytes=64)[:]]
+        y = [by_halves(x) for x in [x[:] for x in tiles("y", last, [P, S], F32)]] + [plain[:, :, 0, :]]
         diff = [x[:] for x in tiles("diff", last, [P, S], F32)]
         low_t = [x[:] for x in tiles("low_t", 2, [P, S], F32)]
         rise_t = [x[:] for x in tiles("rise_t", 2, [P, S], F32)]
@@ -150,7 +145,7 @@ def tile_picked_ppo8_none_po_kernel(tc, x_words, x_scales, w1, old, adv, offs, s
         for r in range(PACK):
             nc.scalar.dma_start(xg_scales[r:P:QUADRANT, :].bitcast(I32), picked_scales[SPREAD * r : P : QUADRANT, :].bitcast(I32))
         adv_sb.append(load_into_slot("xs", adv_rows[:, 2, :]))
-        xg_words = sb.tile([P, S], U32, name="xg_words", align_bytes=64)
+        xg_words = w_pool.tile([P, S], U32, name="xg_words", align_bytes=64, offset=0)
 
         w_bf = sb.tile([P, PACK * N], BF16, name="w_bf", align_bytes=64)
         w_dealt = w_bf[:].rearrange("p (t m j) -> p m j t", t=PACK, j=PACK)
@@ -177,11 +172,17 @@ def tile_picked_ppo8_none_po_kernel(tc, x_words, x_scales, w1, old, adv, offs, s
             )
             nc.scalar.copy(y[t][:, h, :], by_halves(bank)[:, h, :])
 
-        fetch_adv(1)
-        for t in range(2):
-            make_cap_terms(t)
-            make_low(t)
-        adv_sb.append(load_into_slot("w_raw", adv_rows[:, last, :]))
+        make_cap_terms(0)
+        make_low(0)
+        a.append(sb.tile([P, S], F32, name="a", align_bytes=64)[:])
+        nc.scalar.activation(a[1], adv_sb[1][:].indirect(st_sb[:]), ACT.Copy)
+        make_cap_terms(1)
+        make_low(1)
+        late_a_rows = sb.tile([P, 2, S], F32, name="a", align_bytes=64)
+        a.extend(late_a_rows[:, i, :] for i in range(2))
+        nc.scalar.activation(a[2][:, halves[0]], adv_sb[2][:].indirect(st_sb[:, list_halves[0]]), ACT.Copy)
+        adv_sb.append(w_pool.tile([P, U], F32, name="adv_sb3", align_bytes=64, offset=4 * S))
+        nc.sync.dma_start(adv_sb[last][:], adv_rows[:, last, :])
         old_sb = [load_into_slot(slot, old_rows[:, t, :]) for t, slot in enumerate(("adv_sb1", "w_bf", "picked_scales", "xw"))]
         project(0, psum.tile([P, S], F32, name="a_t", bufs=A_T_BANKS)[:], slice(0, 1))
         for t in range(PACK):
@@ -203,15 +204,14 @@ def tile_picked_ppo8_none_po_kernel(tc, x_words, x_scales, w1, old, adv, offs, s
         whole = slice(0, HALF)
         parts = [slice(0, HALF // 2), slice(HALF // 2, HALF)]
 
-        fetch_adv(2)
-        nc.vector.tensor_copy(a[last][:, halves[0]], adv_sb[last][:].indirect(st_sb[:, list_halves[0]]))
+        nc.vector.tensor_copy(a[2][:, halves[1]], adv_sb[2][:].indirect(st_sb[:, list_halves[1]]))
+        fetch_adv(last)
         for i in range(2):
             make_late_a_cap(i)
         for h in range(2):
             for t in range(2):
                 add_back(cap[0][h][:, t, :], low_t[t][:, halves[h]], rise_t[t][:, halves[h]])
         fetch_old(0)
-        nc.scalar.activation(a[last][:, halves[1]], adv_sb[last][:].indirect(st_sb[:, list_halves[1]]), ACT.Copy)
         b_t = turn_half([2, last], 1)
         for t in range(1, last):
             fetch_old(t)

@@ -76,15 +76,16 @@ def tile_picked_ppo8_none_po_kernel(tc, x_words, x_scales, w1, old, adv, offs, s
         def by_halves(ap):
             return ap.rearrange("p (h c) -> p h c", h=2)
 
-        plain = sb.tile([P, 2, PACK, HALF], F32, name="plain", align_bytes=64)
+        late = sb.tile([P, 2, S + PACK * HALF], F32, name="late", align_bytes=64)
+        plain = late[:, :, S:].rearrange("p h (t c) -> p h t c", t=PACK)
+        b_low, b_rise = late[:, 0, 0:S], late[:, 1, 0:S]
         a = [sb.tile([P, S], F32, name="a", align_bytes=64)[:]]
-        y = [by_halves(x) for x in [x[:] for x in tiles("y", last, [P, S], F32)]] + [plain[:, :, 0, :]]
+        y = [by_halves(x) for x in [x[:] for x in tiles("y", last, [P, S], F32)]] + [late[:, :, S - HALF // 2 : S + HALF // 2]]
         diff = [x[:] for x in tiles("diff", last, [P, S], F32)]
         low_t = [x[:] for x in tiles("low_t", 2, [P, S], F32)]
         rise_t = [x[:] for x in tiles("rise_t", 2, [P, S], F32)]
         a_terms = tiles("a_terms", 2, [P, S], F32)
-        b_terms = sb.tile([P, 2 * S], F32, name="b_terms", align_bytes=64)
-        last_diff = [b_terms[:, 0:HALF], b_terms[:, S : S + HALF]]
+        last_diff = [x[:] for x in tiles("last_diff", 2, [P, HALF], F32)]
         cap = [[psum.tile([P, 2, HALF], F32, name="cap%d%d" % (pair, h)) for h in range(2)] for pair in range(2)]
         low = [psum.tile([P, 2, HALF], F32, name="low%d" % h) for h in range(2)]
         blocks = [slice(c * P, (c + 1) * P) for c in range(S // P)]
@@ -216,10 +217,10 @@ def tile_picked_ppo8_none_po_kernel(tc, x_words, x_scales, w1, old, adv, offs, s
         for t in range(1, last):
             fetch_old(t)
         fetch_last_old(0)
-        nc.scalar.activation(b_terms[:, 0:S], b_t[:], ACT.Copy, scale=CLIP_LO)
+        nc.scalar.activation(b_low, b_t[:], ACT.Copy, scale=CLIP_LO)
         fetch_last_old(1)
-        nc.scalar.activation(b_terms[:, S : 2 * S], b_t[:], ACT.Relu, scale=CLIP_HI - CLIP_LO)
-        add_back(cap[1][1][:].rearrange("p i c -> p (i c)"), b_terms[:, 0:S], b_terms[:, S : 2 * S])
+        nc.scalar.activation(b_rise, b_t[:], ACT.Relu, scale=CLIP_HI - CLIP_LO)
+        add_back(cap[1][1][:].rearrange("p i c -> p (i c)"), b_low, b_rise)
         for h in range(2):
             nc.vector.scalar_tensor_tensor(
                 plain[:, h, 0:2, :], low[h][:], 1.0 / CLIP_LO, first_ratio[:, :, halves[h]], ALU.mult, ALU.mult

@@ -242,15 +242,16 @@ def tile_picked_ppo8_none_po_kernel(tc, x_words, x_scales, w1, old, adv, offs, s
         scales = sb.tile([P, S], U8, name="scales", align_bytes=64)
         words_out = out_1[0].rearrange("p c r -> p (c r)").bitcast(I32)
 
-        def round_and_weave(copy, h, part):
+        def round_and_weave(copy, h, part, rows):
             copy(
-                res_bf[h][:, part, :].rearrange("p (c i) t -> p c t i", i=LINE),
-                res[:, h, :, part].rearrange("p t (c i) -> p c t i", i=LINE),
+                res_bf[h][:, part, rows].rearrange("p (c i) t -> p c t i", i=LINE),
+                res[:, h, rows, part].rearrange("p t (c i) -> p c t i", i=LINE),
             )
 
-        round_and_weave(nc.scalar.copy, 0, whole)
-        round_and_weave(nc.vector.tensor_copy, 1, parts[1])
-        round_and_weave(nc.scalar.copy, 1, parts[0])
+        round_and_weave(nc.scalar.copy, 0, whole, slice(0, PACK))
+        for pair in range(2):
+            round_and_weave(nc.vector.tensor_copy, 1, parts[1], slice(2 * pair, 2 * pair + 2))
+        round_and_weave(nc.scalar.copy, 1, parts[0], slice(0, PACK))
         for h in range(2):
             nc.vector.quantize_mx(
                 out=codes[h][:].bitcast(FP8X4),

@@ -252,12 +252,13 @@ def tile_picked_ppo8_none_po_kernel(tc, x_words, x_scales, w1, old, adv, offs, s
         for pair in range(2):
             round_and_weave(nc.vector.tensor_copy, 1, parts[1], slice(2 * pair, 2 * pair + 2))
         round_and_weave(nc.scalar.copy, 1, parts[0], slice(0, PACK))
-        for h in range(2):
-            nc.vector.quantize_mx(
-                out=codes[h][:].bitcast(FP8X4),
-                scales=scales[:, halves[h]],
-                in_=res_bf[h][:].rearrange("p c t -> p (c t)"),
-            )
+        for h, pieces in ((0, [whole]), (1, parts[::-1])):
+            for part in pieces:
+                nc.vector.quantize_mx(
+                    out=codes[h][:, part].bitcast(FP8X4),
+                    scales=scales[:, halves[h]][:, part],
+                    in_=res_bf[h][:, part, :].rearrange("p c t -> p (c t)"),
+                )
             nc.sync.dma_start(words_out[:, halves[h]], codes[h][:].bitcast(I32))
         for r in range(PACK):
             queue = nc.scalar if r % 2 else nc.sync

@@ -261,5 +261,4 @@ def tile_picked_ppo8_none_po_kernel(tc, x_words, x_scales, w1, old, adv, offs, s
                 )
             nc.sync.dma_start(words_out[:, halves[h]], codes[h][:].bitcast(I32))
         for r in range(PACK):
-            queue = nc.scalar if r % 2 else nc.sync
-            queue.dma_start(out_2[0].bitcast(I32)[r : N // 32 : PACK, :], scales[r:P:QUADRANT, :].bitcast(I32))
+            nc.sync.dma_start(out_2[0].bitcast(I32)[r : N // 32 : PACK, :], scales[r:P:QUADRANT, :].bitcast(I32))

from contextlib import ExitStack

import concourse.mybir as mybir
from concourse.masks import make_identity

K, T, S, N, U = 512, 2048, 512, 512, 1024
FLOPS = 2 * K * N * S

F32 = mybir.dt.float32
BF16 = mybir.dt.bfloat16
I32 = mybir.dt.int32
U32 = mybir.dt.uint32
U16 = mybir.dt.uint16
U8 = mybir.dt.uint8
FP8X4 = mybir.dt.float8_e4m3fn_x4
ALU = mybir.AluOpType
ACT = mybir.ActivationFunctionType

P = 128
PACK = 4
QUADRANT = 32
GROUP = 16
SPREAD = 8
HALF = S // 2
LINE = 4
A_T_BANKS = 2
CLIP_LO, CLIP_HI = 0.8, 1.25
RATIO_SCALE = 0.25


def tile_picked_ppo8_none_po_kernel(tc, x_words, x_scales, w1, old, adv, offs, st, out_0, out_1, out_2):
    nc = tc.nc
    with ExitStack() as ctx:
        sb = ctx.enter_context(tc.tile_pool(name="sb", bufs=1))
        psum = ctx.enter_context(tc.psum_pool(name="psum", bufs=1))

        def tiles(name, count, shape, dtype):
            return [sb.tile(shape, dtype, name="%s%d" % (name, i), align_bytes=64) for i in range(count)]

        halves = [slice(h * HALF, (h + 1) * HALF) for h in range(2)]
        list_halves = [slice(h * HALF // GROUP, (h + 1) * HALF // GROUP) for h in range(2)]

        offs_sb = sb.tile([P, S // GROUP], U16, name="offs_sb")
        st_sb = sb.tile([P, S // GROUP], U16, name="st_sb")
        xw = sb.tile([P, T], U32, name="xw", align_bytes=64)
        xs = sb.tile([P, T], U8, name="xs", align_bytes=64)
        w_pool = ctx.enter_context(tc.tile_pool(name="w_pool", bufs=1))
        w_raw = w_pool.tile([P, PACK, N], F32, name="w_raw", align_bytes=64, offset=0)
        adv_sb = tiles("adv_sb", 2, [P, U], F32)

        adv_rows = adv.rearrange("(p t) u -> p t u", t=PACK)
        old_rows = old.rearrange("(p t) u -> p t u", t=PACK)
        w_rows = w1.rearrange("(p j) c -> p j c", j=PACK)
        out_rows = out_0.rearrange("(p t) j -> p t j", t=PACK)

        warm = sb.tile([P, 2], F32, name="warm")
        nc.gpsimd.memset(warm[:, 0:1], 0.0)
        nc.scalar.activation(warm[:, 1:2], warm[:, 0:1], ACT.Exp)
        xs_words = xs[:].bitcast(I32)
        nc.gpsimd.memset(xs_words[:, 0 : T // 8], 0)
        nc.vector.memset(xs_words[:, T // 8 : T // 4], 0)
        ident = sb.tile([P, P], F32, name="ident", align_bytes=64)
        make_identity(nc, ident[:])

        nc.sync.dma_start(adv_sb[0][:], adv_rows[:, 0, :])
        nc.sync.dma_start(st_sb[:], st)
        nc.sync.dma_start(offs_sb[:], offs)
        nc.sync.dma_start(xs[0:P:SPREAD, :].bitcast(I32), x_scales[0].bitcast(I32))
        nc.sync.dma_start(w_raw[:], w_rows)
        nc.sync.dma_start(adv_sb[1][:], adv_rows[:, 1, :])
        nc.sync.dma_start(xw[:].bitcast(I32), x_words[0].rearrange("p c r -> p (c r)").bitcast(I32))

        last = PACK - 1
        res = sb.tile([P, 2, PACK, HALF], F32, name="res", align_bytes=64)

        def by_halves(ap):
            return ap.rearrange("p (h c) -> p h c", h=2)

        late = sb.tile([P, 2, S + PACK * HALF], F32, name="late", align_bytes=64)
        plain = late[:, :, S:].rearrange("p h (t c) -> p h t c", t=PACK)
        b_low, b_rise = late[:, 0, 0:S], late[:, 1, 0:S]
        a = [sb.tile([P, S], F32, name="a", align_bytes=64)[:]]
        y = [by_halves(x) for x in [x[:] for x in tiles("y", last, [P, S], F32)]] + [late[:, :, S - HALF // 2 : S + HALF // 2]]
        diff = [x[:] for x in tiles("diff", last, [P, S], F32)]
        low_t = [x[:] for x in tiles("low_t", 2, [P, S], F32)]
        rise_t = [x[:] for x in tiles("rise_t", 2, [P, S], F32)]
        a_terms = tiles("a_terms", 2, [P, S], F32)
        last_diff = [x[:] for x in tiles("last_diff", 2, [P, HALF], F32)]
        cap = [[psum.tile([P, 2, HALF], F32, name="cap%d%d" % (pair, h)) for h in range(2)] for pair in range(2)]
        low = [psum.tile([P, 2, HALF], F32, name="low%d" % h) for h in range(2)]
        blocks = [slice(c * P, (c + 1) * P) for c in range(S // P)]

        def fetch_adv(t):
            nc.vector.tensor_copy(a[t], adv_sb[t][:].indirect(st_sb[:]))

        def load_into_slot(slot, rows):
            window = sb.tile([P, U], F32, name=slot, align_bytes=64)
            nc.sync.dma_start(window[:], rows)
            return window

        def turn(t):
            a_t = psum.tile([P, S], F32, name="a_t", bufs=A_T_BANKS)
            for b in blocks:
                nc.tensor.transpose(a_t[:, b], a[t][:, b], ident[:])
            return a_t

        def make_terms(low_term, rise_term, a_t):
            nc.scalar.activation(low_term, a_t, ACT.Copy, scale=CLIP_LO)
            nc.scalar.activation(rise_term, a_t, ACT.Relu, scale=CLIP_HI - CLIP_LO)

        def make_cap_terms(t):
            make_terms(low_t[t], rise_t[t], turn(t)[:])

        def half_blocks(h):
            return [(slice(c * P, (c + 1) * P), slice(h * HALF + c * P, h * HALF + (c + 1) * P)) for c in range(HALF // P)]

        def add_back(bank, low_term, rise_term):
            pieces = [slice(c, c + P) for c in range(0, bank.shape[1], P)]
            for b in pieces:
                nc.tensor.matmul(bank[:, b], low_term[:, b], ident[:], start=b == pieces[0], stop=False, is_transpose=True)
            for b in pieces:
                nc.tensor.matmul(bank[:, b], rise_term[:, b], ident[:], start=False, stop=b == pieces[-1], is_transpose=True)

        def turn_half(tiles_turned, h):
            a_t = psum.tile([P, S], F32, name="a_t", bufs=A_T_BANKS)
            for i, t in enumerate(tiles_turned):
                for place, b in half_blocks(h):
                    nc.tensor.transpose(a_t[:, halves[i]][:, place], a[t][:, b], ident[:])
            return a_t

        def make_late_a_cap(i):
            terms = [a_terms[i][:, c] for c in halves]
            make_terms(terms[0], terms[1], turn_half([2 + i], 0)[:, halves[0]])
            add_back(cap[1][0][:, i, :], terms[0], terms[1])

        def make_low(t):
            for h in range(2):
                for place, b in half_blocks(h):
                    nc.tensor.transpose(low[h][:, t, place], low_t[t][:, b], ident[:])

        nc.scalar.activation(a[0], adv_sb[0][:].indirect(st_sb[:]), ACT.Copy)
        picked_scales = sb.tile([P, S], U8, name="picked_scales", align_bytes=64)
        xg_scales = sb.tile([P, S], U8, name="xg_scales", align_bytes=64)
        nc.gpsimd.memset(xg_scales[:].bitcast(I32), 0)
        nc.vector.tensor_copy(picked_scales[:], xs[:].indirect(offs_sb[:]))
        for r in range(PACK):
            nc.scalar.dma_start(xg_scales[r:P:QUADRANT, :].bitcast(I32), picked_scales[SPREAD * r : P : QUADRANT, :].bitcast(I32))
        adv_sb.append(load_into_slot("xs", adv_rows[:, 2, :]))
        xg_words = w_pool.tile([P, S], U32, name="xg_words", align_bytes=64, offset=0)

        w_bf = sb.tile([P, PACK * N], BF16, name="w_bf", align_bytes=64)
        w_dealt = w_bf[:].rearrange("p (t m j) -> p m j t", t=PACK, j=PACK)
        w_plain = w_raw[:].rearrange("p j (m t) -> p m j t", t=PACK)
        nc.vector.tensor_copy(w_dealt, w_plain)
        w_codes = sb.tile([P, N], U32, name="w_codes", align_bytes=64)
        w_scales = sb.tile([P, N], U8, name="w_scales", align_bytes=64)
        nc.vector.quantize_mx(out=w_codes[:].bitcast(FP8X4), scales=w_scales[:], in_=w_bf[:])
        for h in range(2):
            nc.vector.tensor_copy(xg_words[:, halves[h]], xw[:].indirect(offs_sb[:, list_halves[h]]))


        def project(t, bank, h):
            picked = slice(h.start * HALF, h.stop * HALF)
            cols = slice(t * P, (t + 1) * P)
            nc.tensor.matmul_mx(
                out=bank[:, picked],
                lhsT=w_codes[:, cols].bitcast(FP8X4),
                lhsT_scale=w_scales[:, cols],
                rhs=xg_words[:, picked].bitcast(FP8X4),
                rhs_scale=xg_scales[:, picked],
                start=True,
                stop=True,
            )
            nc.scalar.copy(y[t][:, h, :], by_halves(bank)[:, h, :])

        make_cap_terms(0)
        make_low(0)
        a.append(sb.tile([P, S], F32, name="a", align_bytes=64)[:])
        nc.scalar.activation(a[1], adv_sb[1][:].indirect(st_sb[:]), ACT.Copy)
        make_cap_terms(1)
        make_low(1)
        late_a_rows = sb.tile([P, 2, S], F32, name="a", align_bytes=64)
        a.extend(late_a_rows[:, i, :] for i in range(2))
        nc.scalar.activation(a[2][:, halves[0]], adv_sb[2][:].indirect(st_sb[:, list_halves[0]]), ACT.Copy)
        adv_sb.append(w_pool.tile([P, U], F32, name="adv_sb3", align_bytes=64, offset=4 * S))
        nc.sync.dma_start(adv_sb[last][:], adv_rows[:, last, :])
        old_sb = [load_into_slot(slot, old_rows[:, t, :]) for t, slot in enumerate(("adv_sb1", "w_bf", "picked_scales", "xw"))]
        project(0, psum.tile([P, S], F32, name="a_t", bufs=A_T_BANKS)[:], slice(0, 1))
        for t in range(PACK):
            project(t, cap[t // 2][t % 2][:].rearrange("p i c -> p (i c)"), slice(1 if t == 0 else 0, 2))

        first_ratio = sb.tile([P, 2, S], F32, name="first_ratio", align_bytes=64)
        late_ratio = res[:, 1, :, :].rearrange("p (h i) c -> p h i c", h=2)
        ratio = [by_halves(first_ratio[:, i, :]) for i in range(2)] + [late_ratio[:, :, i, :] for i in range(2)]

        def fetch_old(t):
            nc.vector.tensor_tensor(diff[t], old_sb[t][:].indirect(st_sb[:]), y[t].rearrange("p h c -> p (h c)"), ALU.subtract)
            nc.scalar.activation(ratio[t], by_halves(diff[t]), ACT.Exp, scale=-RATIO_SCALE)

        def fetch_last_old(h):
            window = old_sb[last][:].indirect(st_sb[:, list_halves[h]])
            nc.vector.tensor_tensor(last_diff[h], window, y[last][:, h, :], ALU.subtract)
            nc.scalar.activation(ratio[last][:, h, :], last_diff[h], ACT.Exp, scale=-RATIO_SCALE)

        whole = slice(0, HALF)
        parts = [slice(0, HALF // 2), slice(HALF // 2, HALF)]

        nc.vector.tensor_copy(a[2][:, halves[1]], adv_sb[2][:].indirect(st_sb[:, list_halves[1]]))
        fetch_adv(last)
        for i in range(2):
            make_late_a_cap(i)
        for h in range(2):
            for t in range(2):
                add_back(cap[0][h][:, t, :], low_t[t][:, halves[h]], rise_t[t][:, halves[h]])
        fetch_old(0)
        b_t = turn_half([2, last], 1)
        for t in range(1, last):
            fetch_old(t)
        fetch_last_old(0)
        nc.scalar.activation(b_low, b_t[:], ACT.Copy, scale=CLIP_LO)
        fetch_last_old(1)
        nc.scalar.activation(b_rise, b_t[:], ACT.Relu, scale=CLIP_HI - CLIP_LO)
        add_back(cap[1][1][:].rearrange("p i c -> p (i c)"), b_low, b_rise)
        for h in range(2):
            nc.vector.scalar_tensor_tensor(
                plain[:, h, 0:2, :], low[h][:], 1.0 / CLIP_LO, first_ratio[:, :, halves[h]], ALU.mult, ALU.mult
            )
        for h, part in ((0, whole), (1, parts[0]), (1, parts[1])):
            nc.gpsimd.tensor_tensor(
                plain[:, h, 2:PACK, part], late_ratio[:, h, :, part], late_a_rows[:, :, halves[h]][:, :, part], ALU.mult
            )

        for h in range(2):
            for pair in range(2):
                rows = slice(2 * pair, 2 * pair + 2)
                for part in parts if (h, pair) == (1, 1) else [whole]:
                    nc.vector.tensor_tensor(res[:, h, rows, part], cap[pair][h][:, :, part], plain[:, h, rows, part], ALU.min)
                nc.sync.dma_start(out_rows[:, rows, halves[h]], res[:, h, rows, :])

        res_bf = tiles("res_bf", 2, [P, HALF, PACK], BF16)
        codes = tiles("codes", 2, [P, HALF], U32)
        scales = sb.tile([P, S], U8, name="scales", align_bytes=64)
        words_out = out_1[0].rearrange("p c r -> p (c r)").bitcast(I32)

        def round_and_weave(copy, h, part, rows):
            copy(
                res_bf[h][:, part, rows].rearrange("p (c i) t -> p c t i", i=LINE),
                res[:, h, rows, part].rearrange("p t (c i) -> p c t i", i=LINE),
            )

        round_and_weave(nc.scalar.copy, 0, whole, slice(0, PACK))
        for pair in range(2):
            round_and_weave(nc.vector.tensor_copy, 1, parts[1], slice(2 * pair, 2 * pair + 2))
        round_and_weave(nc.scalar.copy, 1, parts[0], slice(0, PACK))
        for h, pieces in ((0, [whole]), (1, parts[::-1])):
            for part in pieces:
                nc.vector.quantize_mx(
                    out=codes[h][:, part].bitcast(FP8X4),
                    scales=scales[:, halves[h]][:, part],
                    in_=res_bf[h][:, part, :].rearrange("p c t -> p (c t)"),
                )
            nc.sync.dma_start(words_out[:, halves[h]], codes[h][:].bitcast(I32))
        for r in range(PACK):
            nc.sync.dma_start(out_2[0].bitcast(I32)[r : N // 32 : PACK, :], scales[r:P:QUADRANT, :].bitcast(I32))
